import numpy as np, ml_dtypes
CORES = [25,29,65,69,153,157,193,197]
N = 8
BF = ml_dtypes.bfloat16
V, W, P, CAP, RO = 512, 4096, 2, 48, 2
def mates(rng):
    o = np.argsort(rng.random((8, 16, W)), axis=-1); m = np.zeros((8, 16, W), np.int64)
    np.put_along_axis(m, o[..., 0::2], o[..., 1::2], -1); np.put_along_axis(m, o[..., 1::2], o[..., 0::2], -1)
    return m, o
def cliques(rng, s, who):
    i = 0
    while i < len(who):
        m = int(rng.integers(2, 10)); c = who[i:i + m]; m = len(c); i += m
        if m > 1: s[np.argsort(rng.random((m, 16)), axis=1)[:, :m - 1], c[:, None]] = c[(np.arange(m)[:, None] + 1 + np.arange(m - 1)) % m]
def net(rng):
    m, o = mates(rng); keep = rng.choice(np.array([0.0, 0.1, 0.25, 0.4, 0.6, 1.0]), (8, 1, W))
    s = np.where(rng.random(m.shape) < keep, m, W); twins = []
    for g in range(8):
        i = rng.permutation(W // 2)[:W // 16]; v = o[g, 0, 2 * i]; b = o[g, 0, 2 * i + 1]
        s[g][:, b] = m[g][:, b]; s[g][0, b] = rng.integers(0, W, len(b)); s[g][0, v] = b
        who = rng.permutation(np.setdiff1d(np.arange(W), np.concatenate([v, b])))[:W // 8]
        s[g][:, who] = W; cliques(rng, s[g], who); twins.append((v, b))
    return s, twins
def pack(x, s):
    cut = lambda a: np.ascontiguousarray(a.reshape(8, 16, N, V).transpose(2, 0, 1, 3).reshape(N, 128, V))
    return {"x": cut(x).astype(np.float32).astype(BF), "stars": cut(s).astype(np.int32)}
def same(x, twins):
    for g in range(8): x[g][:, twins[g][0]] = x[g][:, twins[g][1]]
    return x
def setup_inputs(rng):
    s, twins = net(rng)
    return pack(same(rng.integers(0, 256, (8, 16, W)), twins), s)
def full(rng, s, x):
    a = int(rng.integers(0, N)); v = np.concatenate([q * V + rng.permutation(np.arange(0, V, P))[:CAP] for q in range(N)])
    b = rng.permutation(np.setdiff1d(np.arange(a * V, (a + 1) * V), v))[:N * CAP]
    s[0, v] = b; s[10, v] = rng.choice(np.setdiff1d(np.arange(W), np.concatenate([v, b])), len(v))
def far(rng, s, x):
    o = rng.permutation(W); v = o[o % P == 0][:CAP]; rest = o[~np.isin(o, v)]; b = rest[:CAP]; e = rest[CAP:2 * CAP]; i = np.arange(CAP) & 3
    low = rng.integers(1, 16, (16, CAP)); high = rng.integers(240, 253, (16, CAP))
    high[0] += (np.where(i == 2, 3, 1) - np.add.reduce(high - low, axis=0)) & 3
    near = low.copy(); near[1] += 1; near[2] -= (i == 2).astype(np.int64)
    x[:, b] = low; x[:, v] = np.where(i == 3, near, high); x[:, e] = np.where(i == 3, high, near)
    s[rng.integers(0, 16, CAP), v] = b; m = i > 0; s[8, b[m]] = e[m]; s[0, e[m]] = b[m]
    cliques(rng, s, rest[2 * CAP:])
def again(rng, s, x):
    ends = np.array([0, V - 2, V - 1]); o = [q * V + rng.permutation(np.arange(1, V - 2)) for q in range(N)]
    v = [a[a % P == 0][:CAP] for a in o]; rest = [a[~np.isin(a, c)] for a, c in zip(o, v)]
    for q in range(N):
        b = rest[(q + 1) % N][:CAP]; s[rng.integers(0, 16, CAP), v[q]] = b; x[:, b] = x[:, v[q]]
        s[rng.integers(0, 16, 3), q * V + ends] = rest[(q + 2) % N][CAP:CAP + 3]
        cliques(rng, s, rest[q][CAP + 3:])
def setup_inputs_room(rng):
    s = np.full((8, 16, W), W, np.int64); cyc = (CAP, CAP + 1, CAP - 1, 1, 0); rows = np.arange(16)[:, None]
    x = rng.integers(0, 256, (8, 16, W)); kind = rng.permutation(8)
    for g in range(8):
        if kind[g] > 4:
            (full, far, again)[int(kind[g]) - 5](rng, s[g], x[g])
            continue
        talk = np.zeros(W, bool); to = []
        for q in range(N):
            act = rng.permutation(np.arange(0, V, P)); left = 3 * len(act) // 4; pos = 0
            for d in [0] + list(range(1, N)):
                n = min(cyc[(d - 1 + int(kind[g])) % 5], left - pos); v = q * V + act[pos:pos + n]; pos += n
                talk[v] = True; to.append((v, (q + d) % N))
        rest = rng.permutation(np.flatnonzero(~talk)); cliques(rng, s[g], rest)
        for v, a in to:
            n = len(v); b = rng.choice(rest[rest // V == a], n); k = rng.integers(0, 16, n)
            s[g][:, v] = np.where(rows == k, b, np.where((rows > k) & (rng.random((16, n)) < 0.4), rng.integers(0, W, (16, n)), W))
    return pack(x, s)
def setup_inputs_ties(rng):
    m, o = mates(rng); s = np.where(rng.random(m.shape) < rng.choice(np.array([0.1, 0.4, 0.9, 1.0]), (8, 1, W)), m, W)
    n = rng.permutation(np.array([1, 1, 2, 2, 2, 3, 3, 4]))[:, None, None]
    x = rng.integers(0, 252, (8, 16, 1)) + (rng.random((8, 16, W)) * n).astype(np.int64)
    return pack(x, s)
def setup_inputs_alike(rng):
    s, o = mates(rng); kind = rng.permutation(8) & 3
    for g in range(8):
        q = int(rng.integers(0, N))
        if kind[g] == 0: s[g] = rng.choice(np.array([0, V - 1, V, W - 1]), (16, W))
        elif kind[g] == 1: s[g] = rng.integers(q * V, (q + 1) * V, (16, W))
        elif kind[g] == 2: s[g, 1::2] = s[g, 0::2]; s[g, 4] = np.arange(W)
        else: s[g] = np.repeat(s[g, :1], 16, axis=0); s[g][:, q * V:(q + 1) * V] = W
    s = np.where(rng.random(s.shape) < rng.choice(np.array([0.3, 0.6, 0.9]), (8, 1, W)), s, W)
    return pack(rng.integers(0, 256, (8, 16, W)), s)
def setup_inputs_line(rng):
    m, o = mates(rng); s = np.where(rng.random(m.shape) < rng.choice(np.array([0.3, 0.7, 1.0]), (8, 1, W)), m, W)
    p = rng.integers(0, 256, (8, 1, W)); x = np.where(rng.random((8, 16, 1)) < 0.5, p, 255 - p)
    for g in range(8):
        i = np.argsort(p[g, 0] + rng.random(W)).reshape(-1, 64); low = i[:, :32].reshape(-1); high = i[:, 32:].reshape(-1)
        up = rng.random(len(low)) < 0.5; v = np.where(up, low, high); b = np.where(up, high, low)
        s[g, 0, v] = b; s[g, 0, b] = rng.integers(0, W, len(b))
    return pack(x, s)
def setup_inputs_spread(rng):
    s, twins = net(rng)
    x = (np.exp2(8 * rng.random((8, 1, W))) * rng.random((8, 16, W)) * (rng.random((8, 1, W)) > 0.0625)).astype(np.int64)
    return pack(same(np.minimum(x, 255), twins), s)
def check_inputs(d):
    bad = []; v = np.asarray(d["x"]).astype(np.float32)
    if not (np.min(v) >= 0 and np.max(v) <= 255 and np.all(v == np.floor(v))): bad.append("x: whole numbers from 0 to 255")
    if np.min(d["stars"]) < 0 or np.max(d["stars"]) > W: bad.append("range of stars")
    return bad
def judge(pts, e, b, z):
    live = e < W; xz = pts[z]; xb = pts[b]; xe = pts[e]
    ez = np.add.reduce(np.abs(xe - xz[:, None, :]), axis=2); eb = np.add.reduce(np.abs(xe - xb[:, None, :]), axis=2)
    zb = np.add.reduce(np.abs(xz - xb), axis=1)
    block = np.any(live & (ez < zb[:, None]), axis=1)
    new = np.where(live & (ez < eb), W, e); free = new == W
    new[np.arange(len(b)), np.argmax(free, axis=1)] = z
    return np.where((~block & np.any(free, axis=1))[:, None], new, e)
def reference(x, stars):
    pts = np.zeros((8, W + 1, 16), np.int64); st = np.full((8, W + 1, 16), W, np.int64)
    pts[:, :W] = x.astype(np.float32).astype(np.int64).reshape(N, 8, 16, V).transpose(1, 0, 3, 2).reshape(8, W, 16)
    st[:, :W] = stars.astype(np.int64).reshape(N, 8, 16, V).transpose(1, 0, 3, 2).reshape(8, W, 16)
    for t in range(RO):
        act = np.flatnonzero((np.arange(W) % V) % P == t % P); src = act // V; ks = (5 * t + np.arange(16)) & 15
        new = st.copy()
        for g in range(8):
            mine = st[g][act]; b = mine[:, ks]; c = mine[:, (ks + 1) & 15]; sb = st[g][b]
            hasv = np.any(sb == act[:, None, None], axis=2); hasc = np.any(sb == c[:, :, None], axis=2)
            one = (b < W) & ~hasv; two = (b < W) & hasv & (c < W) & ~hasc
            some = np.any(one | two, axis=1); j = np.argmax(one | two, axis=1); i = np.arange(len(act))
            to = b[i, j]; z = np.where(one[i, j], act, c[i, j])
            for a in range(N):
                here = some & (to // V == a)
                ix = np.concatenate([np.flatnonzero(here & (src == q))[:CAP] for q in range(N)])
                ix = ix[np.unique(to[ix], return_index=True)[1]]
                new[g, to[ix]] = judge(pts[g], st[g][to[ix]], to[ix], z[ix])
        st = new
    y = st[:, :W].reshape(8, N, V, 16).transpose(1, 0, 3, 2).reshape(N, 128, V)
    return {"y": np.ascontiguousarray(y).astype(np.float32)}

@@ -1,0 +1,565 @@
+import math
+from concourse.bass import DstId, RemoteDMATransfer
+from concourse.mybir import AluOpType, ActivationFunctionType
+
+ALU = AluOpType
+ACT = ActivationFunctionType
+N, W, RO = 8, 4096, 2
+SH = 2048.0
+NCH, U = 4, 64
+BIG, HUGE = 65536.0, 4194304.0
+INVB = 27.0 / 64.0
+LNB = -math.log(INVB)
+MAGIC = 12582912.0
+FAR = 1024.0
+
+SCRATCH = {}
+for _d, _l in (
+    ("int32", "sin 512 pi 16 pj 16 pk 8 ti 160 bti 16 btm 32"),
+    ("float16", "s16 512 pa 1024 la 1024 ha 256 pz 512 lz 512 hz 128 nat0 512 nat1 512 nat2 512 cv 432 wn 512 e16 256"),
+    ("uint16", "off 256 obz 32 eo 256 slot 16 key 32 chi 128 clo 32"),
+    ("float32", "yo 512 sw 4104 nw0 896 nw1 896 dsc 512 gs 4096 ae 256 keep 256 nn 256 ns 2320 dab 256 ssc 256 btf 32 "
+                "wtt 16 lg 288 rr 288 kp 288 ke 288 ks 288 t2 32 t3 32 mf 144 mhi 128 mlo 272 pc 16 plc 16 kmask 16 gmask 8 "
+                "rd 256 fb 32 tf 256"),
+    ("bfloat16", "xin 512 xnat 512 xw 4112 ni 256 za 256 zb 256 dead 256 xbz 512 mzb 256 blk 256 fr 256 ind 256 fac 256 "
+                 "wsel 256 csel 256 ohh 2048 ohl 512 ii 256 ineg 128 ibig 128 jj 128 sg 256 jhi 128 j9 128 jbig 128 "
+                 "jnbig 128 dm 128 shm 128 ish 128 km 256 tmpb 128 lt 256 li 256 wd 144 wd2 144 sel 2048 rep 1024 gsel 8 "
+                 "gx 4096 eqw 4096 eqc 4096 az 4096 ab 4096 pm 512 ck 384 ones 256 zero 256"),
+):
+    _w = _l.split()
+    for _i in range(0, len(_w), 2):
+        SCRATCH[_w[_i]] = ("sbuf", [128, int(_w[_i + 1])], _d)
+SCRATCH["val"] = ("sbuf", [128, 3, 256], "float16")
+SCRATCH["dx"] = ("dram", [16, 4096], "bfloat16")
+for _b in range(8):
+    SCRATCH["pb%d" % _b] = ("psum", [128, 512], "float32")
+SEMAPHORES = ["qv", "qa", "qp", "qg", "lds", "ldx", "arr1", "arr2", "h1", "h2", "sent", "st0", "st1", "dx1", "dx2"]
+QSEM = {"v": "qv", "a": "qa", "p": "qp", "g": "qg"}
+LAT = 110.0
+
+
+def routes(T, topo):
+    out = []
+    for c in T.cores:
+        direct = [r for r, d in enumerate(T.cores) if d != c and topo.may_write(c, d)]
+        rest = [r for r, d in enumerate(T.cores) if d != c and not topo.may_write(c, d)]
+        sets = {}
+        for r in rest:
+            sets.setdefault((topo.host(T.cores[r]), topo.chip(T.cores[r])), []).append(r)
+        hs = [h for h in topo.cores_of(c) if T.rank_of(h) is None and topo.die(h) == topo.die(c)
+              and all(topo.may_write(h, T.cores[r]) for r in rest)]
+        via = [(hs[i], rs) for i, rs in enumerate(sets.values())]
+        for h, rs in via:
+            assert rs == list(range(rs[0], rs[0] + 2))
+        out.append((direct, via))
+    return out
+
+
+def bits(es):
+    m = 0
+    for e in es:
+        m |= 1 << e
+    return m
+
+
+def engine_plan(T, topo, rank, direct, via):
+    c = T.cores[rank]
+    far = [r for r in direct if topo.same_plane(c, T.cores[r])]
+    near = [r for r in direct if r not in far]
+    off = topo.engines(c, T.cores[far[0]])
+    on = [e for e in topo.engines(c, via[0][0]) if e not in off]
+    n, m = len(off) // len(far), len(on) // len(via)
+    plan = {r: off[i * n:(i + 1) * n] for i, r in enumerate(far)}
+    for r in near:
+        plan[r] = on[:m]
+    return plan, [on[i * m:(i + 1) * m] for i in range(len(via))]
+
+
+def helper_engines(T, topo, h, rs):
+    es = topo.engines(h, T.cores[rs[0]])
+    n = len(es) // len(rs)
+    return [es[i * n:(i + 1) * n] for i in range(len(rs))]
+
+
+def dst(topo, d, s):
+    rid, pid = topo.addr(d, s)
+    return DstId(rid=rid, pnc=pid)
+
+
+def helper_program(g, core, T, topo, rank, rs, n_in):
+    es = helper_engines(T, topo, core, rs)
+    for land, to, w, arr, h in ((T.ha, T.la, 128, T.sem.arr1, T.sem.h1), (T.hz, T.lz, 64, T.sem.arr2, T.sem.h2)):
+        g.wait_ge(h, n_in)
+        g.remote_dma_fused([RemoteDMATransfer(dst_ids=[dst(topo, T.cores[r], core)], dma_engine_mask=bits(es[i]), remote_sem=arr,
+                                              src=land[:, i * w:(i + 1) * w], dst=to[:, rank * w:(rank + 1) * w])
+                            for i, r in enumerate(rs)], local_sem=T.sem.sent)
+    g.wait_ge(T.sem.sent, 2 * sum(len(e) for e in es))
+
+
+def build(g, core, T, topo, rank):
+    ops = []
+    state = {}
+    rts = routes(T, topo)
+    direct, via = rts[rank]
+    plan, hplan = engine_plan(T, topo, rank, direct, via)
+    n_arr = 0
+    for s in range(N):
+        if s == rank:
+            continue
+        ds, vs = rts[s]
+        if rank in ds:
+            n_arr += len(engine_plan(T, topo, s, ds, vs)[0][rank])
+        else:
+            h, rs = [e for e in vs if rank in e[1]][0]
+            n_arr += len(helper_engines(T, topo, h, rs)[rs.index(rank)])
+    pb = [T["pb%d" % b] for b in range(8)]
+
+    def op(eng, cost, rd, wr, fn, bank=None, done=None, lag=0.0):
+        me = len(ops)
+        rd, wr = rd.split(), wr.split()
+        deps = set()
+        for k in rd + wr:
+            st = state.setdefault(k, [None, []])
+            if st[0] is not None:
+                deps.add(st[0])
+        for k in wr:
+            deps.update(state[k][1])
+        for k in rd:
+            state[k][1].append(me)
+        for k in wr:
+            state[k] = [me, []]
+        deps.discard(me)
+        ops.append({"eng": eng, "cost": cost, "deps": deps, "fn": fn, "bank": bank, "done": done, "lag": lag, "wr": (wr + ["-"])[0]})
+
+    def vc(n, f=1.0):
+        return 50.0 + max(64.0, n * f)
+
+    def ts(out, in0, s1, s2, o0, o1, n, rd, wr, bank=None, f=1.0):
+        if o1 is None:
+            op("v", vc(n, f), rd, wr, lambda: g.vector.tensor_scalar(out, in0, s1, None, o0), bank)
+        else:
+            op("v", vc(n, f), rd, wr, lambda: g.vector.tensor_scalar(out, in0, s1, s2, o0, o1), bank)
+
+    def tt(out, a, b, o, n, rd, wr, bank=None):
+        op("v", vc(n, 2.0 if bank is None else 1.0), rd, wr, lambda: g.vector.tensor_tensor(out, a, b, o), bank)
+
+    def cp(out, a, n, rd, wr, bank=None, f=1.0):
+        op("v", vc(n, f), rd, wr, lambda: g.vector.tensor_copy(out, a), bank)
+
+    def ms(out, c, n, wr):
+        op("v", vc(n), "", wr, lambda: g.vector.memset(out, c))
+
+    def scan(out, d0, d1, init, o0, o1, n, rd, wr, bank=None, f=1.0):
+        op("v", vc(n, f), rd, wr, lambda: g.vector.tensor_tensor_scan(out, d0, d1, init, o0, o1), bank)
+
+    def act(out, a, func, n, rd, wr, bank=None, f=1.0, bias=0.0, scale=1.0, extra=0.0):
+        op("a", 65.0 + extra + max(64.0, n * f), rd, wr, lambda: g.scalar.activation(out, a, func, bias=bias, scale=scale), bank)
+
+    def iota(out, pat, n, rd, wr, real=True):
+        if real:
+            op("g", 130.0 + 2 * n, rd, wr, lambda: g.iota(out, pat, 0, 0, allow_small_or_imprecise_dtypes=True))
+        else:
+            op("g", 130.0 + 2 * n, rd, wr, lambda: g.iota(out, pat, 0, 0))
+
+    def asel(out, a, pat, o, fill, base, cm, n, rd, wr):
+        op("g", 170.0 + 2 * n, rd, wr, lambda: g.affine_select(out, a, pat, o, fill, base, cm))
+
+    def mm(items, rd, wr, bank):
+        def fn():
+            for o, l, r, s, e, n in items:
+                last = g.tensor.matmul(o, l, r, s, e)
+            return last
+        op("p", 60.0 + 0.5 * sum(max(64, i[5]) for i in items), rd, wr, fn, bank)
+
+    def group(out, terms, n):
+        return [(out, l, r, i == 0, i == len(terms) - 1, n) for i, (l, r) in enumerate(terms)]
+
+    def keys(name, n):
+        return " ".join("%s%d" % (name, i) for i in range(n)) + " "
+
+    def blocks(t, w, n):
+        return [t[:, w * i:w * i + w] for i in range(n)]
+
+    GA, SC = 1.56, 3.8
+    ADD, SUB, MUL, MAX, MIN, EQ = ALU.add, ALU.subtract, ALU.mult, ALU.max, ALU.min, ALU.is_equal
+    op("s", 60.0, "", "sin", lambda: g.sync.dma_start(T.sin[:], T.stars[:]).then_inc(T.sem.lds, 16), done=("lds", 16), lag=2200.0)
+    op("a", 60.0, "", "xin", lambda: g.scalar.dma_start(T.xin[:], T.x[:]).then_inc(T.sem.ldx, 16), done=("ldx", 16), lag=2000.0)
+    ms(T.ones[:], 1.0, 128, "ones")
+    asel(T.ii[:], T.ones[:], [[0, 2], [-1, 128]], EQ, 0.0, 0, 1, 256, "ones", "ii")
+    I = T.ii[:, 0:128]
+    ts(T.s16[:], T.sin[:], -SH, None, ADD, None, 512, "sin", "s16")
+    mm([(pb[0][:, j::4], T.s16[:, 128 * j:128 * j + 128], I, True, True, 128) for j in range(4)], "s16 ii", "b0", 0)
+    mm([(pb[1][:, j::4], T.xin[:, 128 * j:128 * j + 128], I, True, True, 128) for j in range(4)], "xin ii", "b1", 1)
+    cp(T.pa[:, 1::2], pb[1][:], 512, "b1", "pa1", 1)
+    cp(T.pa[:, 0::2], pb[0][:], 512, "b0", "pa0", 0)
+
+    def send(src, land, to, w, hsem, arr):
+        def fn():
+            g.remote_dma_fused([RemoteDMATransfer(dst_ids=[dst(topo, h, core)], dma_engine_mask=bits(hplan[i]), remote_sem=hsem,
+                                                  src=src[:, rs[0] * w:(rs[0] + 2) * w], dst=land[:])
+                                for i, (h, rs) in enumerate(via)], local_sem=T.sem.sent)
+            g.remote_dma_fused([RemoteDMATransfer(dst_ids=[dst(topo, T.cores[r], core)], dma_engine_mask=bits(plan[r]), remote_sem=arr,
+                                                  src=src[:, r * w:(r + 1) * w], dst=to[:, rank * w:(rank + 1) * w])
+                                for r in direct], local_sem=T.sem.sent)
+        return fn
+    n_sent = sum(len(e) for e in hplan) + sum(len(plan[r]) for r in direct)
+    op("g", 1000.0, "pa0 pa1", "sent1", send(T.pa, T.ha, T.la, 128, T.sem.h1, T.sem.arr1), done=())
+    cp(T.la[:, rank * 128:(rank + 1) * 128], T.pa[:, rank * 128:(rank + 1) * 128], 128, "pa0 pa1", "laown", f=0.5)
+    op(None, 6000.0, "sent1", "la", None, done=("arr1", n_arr))
+    op("g", 170.0, "", "pi", lambda: g.iota(T.pi[:], [[1, 16]], 0, 1))
+    iota(T.mlo[:], [[0, 17], [1, 16]], 272, "", "mlo")
+    iota(T.mhi[:], [[1, 8], [0, 16]], 128, "", "mhi")
+    iota(T.mf[:], [[1, 144]], 144, "", "mf")
+    P, PHI, CORB, CORS, NCEN, DV, A48, N48, WQ, WDC, W0, FB0, DV0 = blocks(T.pc, 1, 13)
+    PLO, ORD1 = T.plc[:, 0:1], T.plc[:, 11:12]
+    cp(P, T.pi[:, 0:1], 1, "pi", "P")
+    ts(T.pj[:], T.pi[:], 15, None, ALU.bitwise_and, None, 16, "pi", "pj")
+    cp(T.plc[:], T.pj[:], 16, "pj", "plc")
+    ts(PHI, P, PLO, 0.0625, SUB, MUL, 1, "P plc", "PHI")
+    ts(T.jj[:], T.mhi[:], PHI, None, EQ, None, 128, "mhi PHI", "jj")
+    ts(T.km[:], T.mlo[:, 0:256], PLO, None, EQ, None, 256, "mlo plc", "km")
+    ts(T.gmask[:], T.mf[:, 0:8], PHI, None, EQ, None, 8, "mf PHI", "gmask")
+    ts(T.kmask[:], T.mf[:, 0:16], PLO, None, EQ, None, 16, "mf plc", "kmask")
+    cp(T.gsel[:], T.gmask[:], 8, "gmask", "gsel")
+    REP, SEL, PM, CK = blocks(T.rep, 128, 8), blocks(T.sel, 128, 16), blocks(T.pm, 128, 4), blocks(T.ck, 128, 3)
+    LTS, LIS = blocks(T.lt, 128, 2), blocks(T.li, 128, 2)
+    for r in range(8):
+        act(REP[r], T.km[:, 0:128], ACT.Copy, 128, "km gmask", "rep%d" % r, scale=T.gmask[:, r:r + 1])
+    for k in range(16):
+        ts(SEL[k], T.jj[:], T.kmask[:, k:k + 1], None, MUL, None, 128, "jj kmask", "sel%d" % k, f=0.5)
+    for name, src, c in (("ineg", "ii", -1.0), ("ibig", "ii", 4096.0), ("j9", "jj", 9.0), ("jbig", "jj", 4096.0), ("jnbig", "jj", -4096.0)):
+        act(T[name][:], T[src][:, 0:128], ACT.Copy, 128, src, name, scale=c)
+    for col, name, src, sn, a, b in ((CORS, "CORS", PLO, "plc", -BIG, 15 * BIG - 9.0), (CORB, "CORB", PLO, "plc", -BIG, 15 * BIG - 30 * SH),
+                                     (NCEN, "NCEN", PLO, "plc", -512.0, -255.5 - 30 * SH), (A48, "A48", PHI, "PHI", 48.0, 0.0),
+                                     (N48, "N48", PHI, "PHI", -48.0, 0.0), (WDC, "WDC", PHI, "PHI", 16.0, 15.0),
+                                     (W0, "W0", PHI, "PHI", 512.0, -SH)):
+        ts(col, src, a, b, MUL, ADD, 1, sn, name)
+    ts(FB0, PHI, 48.0, PLO, MUL, ADD, 1, "PHI plc", "FB0")
+    ts(T.pk[:, 0:1], PHI, PLO, 8.0, SUB, ADD, 1, "PHI plc", "pk0")
+    ts(T.pk[:, 1:2], T.pk[:, 0:1], 7, None, ALU.bitwise_and, None, 1, "pk0", "pk1")
+    cp(DV0, T.pk[:, 1:2], 1, "pk1", "DV0")
+    ts(WQ, PLO, 8.0, 8.0, EQ, MUL, 1, "plc", "WQ")
+    ts(DV, DV0, WQ, None, MAX, None, 1, "DV0 WQ", "DV")
+    act(T.dm[:], T.jj[:], ACT.Copy, 128, "jj DV", "dm", scale=DV)
+    ts(T.wd[:], T.mf[:], WDC, None, EQ, None, 144, "mf WDC", "wd")
+    act(T.wd2[:], T.wd[:], ACT.Copy, 144, "wd", "wd2", scale=2.0)
+    ts(T.rd[:], T.km[:], HUGE + BIG, -BIG, MUL, ADD, 256, "km", "rd")
+    act(T.fb[:], T.mf[:, 0:32], ACT.Identity, 32, "mf FB0", "fb", scale=16.0, bias=FB0)
+    ts(T.tmpb[:], T.mlo[:, 0:128], 8.0, -1.0, ALU.is_ge, MUL, 128, "mlo", "tmpb")
+    tt(T.jhi[:], T.tmpb[:], T.jj[:], MUL, 128, "tmpb jj", "jhi")
+    for i in range(4):
+        asel(PM[i], T.ones[:, 0:128], [[-16, 8], [-256, 2], [-1, 8]], EQ, 0.0, 256 * (i % 2) - 8 * (i // 2), 1, 128, "ones sent1", "pm%d" % i)
+    iota(T.tf[:], [[2, 256]], 256, "sent1", "tf")
+    asel(LTS[0], T.jbig[:], [[1, 128]], ALU.is_gt, 0.0, 0, -1, 128, "jbig sent1", "lt0")
+    ts(T.tmpb[:], T.mlo[:, 11:139], ORD1, None, ALU.is_gt, None, 128, "mlo plc", "tmpb")
+    tt(LTS[1], T.tmpb[:], T.jbig[:], MUL, 128, "tmpb jbig", "lt1")
+    for t in range(RO):
+        asel(LIS[t], LTS[t], [[1, 128]], ALU.not_equal, -4096.0, 0, -1, 128, "lt%d sent1" % t, "li%d" % t)
+        ts(T.wn[:, 256 * t:256 * t + 256], T.tf[:], W0, float(t), ADD, ADD, 256, "tf W0", "wn%d" % t)
+    asel(T.shm[:], T.jj[:], [[-1, 128]], EQ, 0.0, -1, 1, 128, "jj sent1", "shm")
+    asel(T.shm[:, 15::16], T.jj[:, 15::16], [[-16, 8]], EQ, 0.0, 0, 1, 8, "jj", "shm")
+    asel(T.ish[:], T.shm[:], [[-1, 128]], ALU.not_equal, 1.0, 0, 1, 128, "shm", "ish")
+    iota(T.ti[:, 0:128], [[512, 8], [1, 16]], 128, "sent1", "ti0", False)
+    iota(T.ti[:, 128:160], [[16, 32]], 32, "sent1", "ti1", False)
+    cp(T.chi[:], T.ti[:, 0:128], 128, "ti0", "chi")
+    cp(T.clo[:], T.ti[:, 128:160], 32, "ti1", "clo")
+    for i, c in enumerate((-16.0, -464.0, 256.0)):
+        ms(CK[i], c, 64, "ck%d" % i)
+    ms(T.zero[:], 0.0, 128, "zero")
+    ms(T.sw[:, 4096:4104], SH, 8, "sw8")
+    ms(T.xw[:, 4096:4112], FAR, 16, "xw8")
+    ms(T.ns[:, 0:432], 0.0, 432, "ns")
+    ONE = T.ones[:, 0:64]
+    R = [T.wd[:, 15 - k:143 - k] for k in range(16)]
+    R2 = R[0:8] + [T.wd2[:, 15 - k:143 - k] for k in range(8, 16)]
+    SW, XW = keys("sw", 9), "xw xw8 "
+    swin, xwin = T.sw[:, 0:4104], T.xw[:, 0:4112]
+    nat = [T.nat0, T.nat1, T.nat2]
+    nw = [T.nw0, T.nw1]
+    mm([(pb[0][:, 128 * j:128 * j + 128], T.la[:, 2 * j::8], I, True, True, 128) for j in range(4)], "la laown ii", "b0", 0)
+    cp(T.nat0[:], pb[0][:], 512, "b0", "nat0", 0)
+    mm([(pb[6][:, 128 * j:128 * j + 128], T.la[:, 2 * j + 1::8], I, True, True, 128) for j in range(4)], "la laown ii", "acce accb accs p12", 6)
+    act(T.xnat[:], pb[6][:], ACT.Copy, 512, "acce accb accs p12", "xnat", 6)
+    act(T.nw0[:, 384:896], pb[0][:], ACT.Copy, 512, "b0 nat0", "nwo0", 0)
+
+    def x_out():
+        for r in range(8):
+            g.sync.dma_start(T.dx[:, 512 * r:512 * r + 512], T.xnat[16 * r:16 * r + 16, :]).then_inc(T.sem.dx1, 16)
+
+    def x_in():
+        for r in range(8):
+            g.sync.dma_start(T.xw[16 * r:16 * r + 16, 0:4096], T.dx[:]).then_inc(T.sem.dx2, 16)
+    op("s", 800.0, "xnat", "dx", x_out, done=("dx1", 128), lag=2500.0)
+    op("s", 800.0, "dx", "xw", x_in, done=("dx2", 128), lag=7000.0)
+
+    def halves(j):
+        return ([slice(1024 * j + 512 * h, 1024 * j + 512 * h + 512) for h in range(2)],
+                [slice(1024 * j + 512 * (k // 8) + k % 8, 1024 * j + 512 * (k // 8) + 512, 8) for k in range(16)])
+
+    for t in range(RO):
+        nk = "nat%d " % t
+        wk = "wn%d " % t
+        LT, LI = LTS[t], LIS[t]
+        for r in range(8):
+            b = [1, 2, 3][r % 3] if t == 0 else (r + 1) % 4
+            mm([(pb[b][:], REP[r], nat[t][:], True, True, 512)], nk + "rep%d" % r, "b%d" % b, b)
+            if r % 2 == 0:
+                act(T.sw[:, 512 * r:512 * r + 512], pb[b][:], ACT.Copy, 512, "b%d" % b, "sw%d" % r, b)
+            else:
+                cp(T.sw[:, 512 * r:512 * r + 512], pb[b][:], 512, "b%d" % b, "sw%d" % r, b)
+        mm(sum([group(pb[7][:, 128 * h:128 * h + 128], [(PM[2 * h + e], nat[t][:, t + 2 * e::4]) for e in range(2)], 128) for h in range(2)], []),
+           keys("pm", 4) + nk, "b7", 7)
+        ts(T.off[:], pb[7][:, 0:256], SH, None, ADD, None, 256, "b7", "off", 7)
+        ts(T.ni[:], nat[t][:, t::2], SH, None, EQ, None, 256, nk, "ni", f=0.5)
+        fill = [0]
+        for j in range(NCH):
+            u = slice(U * j, U * j + U)
+            c = "%d " % j
+            hs, ks = halves(j)
+            sa = nat[t][:, t + 2 * U * j:2 * U * (j + 1):2]
+            wn = T.wn[:, 256 * t + U * j:256 * t + U * j + U]
+            za, zb = T.za[:, u], T.zb[:, u]
+            for h in range(2):
+                act(T.gs[:, hs[h]], swin.indirect(T.off[:, 128 * h + 32 * j:128 * h + 32 * j + 32]), ACT.Copy, 512, SW + "off", "gs%d%d" % (j, h), f=GA)
+            b = fill[0] % 2
+            fill[0] += 1
+            mm([(pb[b][:, k::8], I, wn, True, True, U) for k in range(8)], "ii " + wk, "b%d" % b, b)
+            for h in range(2):
+                tt(T.eqw[:, hs[h]], T.gs[:, hs[h]], pb[b][:], EQ, 512, "gs%d%d b%d" % (j, h, b), "eqw%d%d" % (j, h), b)
+            mm(group(pb[4][:, 0:64], [(I, T.ni[:, u])] + [(R[k], T.eqw[:, ks[k]]) for k in range(16)], U),
+               "eqw%d0 eqw%d1 wd ni" % (j, j), "h", 4)
+            ts(za, pb[4][:, 0:64], 0.0, None, EQ, None, U, "h", "za" + c, 4)
+            for h in range(2):
+                b = fill[0] % 2
+                fill[0] += 1
+                mm([(pb[b][:, k::8], SEL[(8 * h + k + 1) % 16], sa, True, True, U) for k in range(8)], keys("sel", 16) + nk, "b%d" % b, b)
+                tt(T.eqc[:, hs[h]], T.gs[:, hs[h]], pb[b][:], EQ, 512, "gs%d%d b%d" % (j, h, b), "eqc%d%d" % (j, h), b)
+            mm(group(pb[4][:, 64:128], [(T.ish[:], T.ni[:, u]), (I, za)] + [(R[k], T.eqc[:, ks[k]]) for k in range(16)], U),
+               "eqc%d0 eqc%d1 wd ni ish za%d" % (j, j, j), "h2", 4)
+            ts(zb, pb[4][:, 64:128], 0.0, None, EQ, None, U, "h2", "zb" + c, 4)
+            mm(group(pb[4][:, 128:192], [(I, sa), (LI, za), (LI, zb)], U) + group(pb[4][:, 192:256], [(I, wn), (LI, za), (LT, zb)], U)
+               + group(pb[4][:, 256:320], [(T.shm[:], sa), (LT, za), (LI, zb)], U),
+               nk + wk + "za%d zb%d lt%d li%d shm" % (j, j, t, t), "p", 4)
+            ts(T.val[:, :, u], pb[4][:, 128:320], 4096.0, SH, ADD, MIN, 192, "p", "val" + c, 4)
+            mm(group(pb[5][:, 128 * j:128 * j + 64], [(CK[2], ONE), (T.jj[:], T.val[:, 0, u])], U)
+               + group(pb[5][:, 128 * j + 64:128 * j + 128], [(T.jj[:], T.val[:, 1, u]), (T.jj[:], T.val[:, 2, u])], U),
+               "jj ck2 ones val" + c, "bz" + c, 5)
+            scan(T.dsc[:, 128 * j:128 * j + 128], T.rd[:, 0:128], pb[5][:, 128 * j:128 * j + 128], 0.0, ADD, MIN, 128, "rd bz" + c, "dsc" + c, 5)
+            ts(T.obz[:, 8 * j:8 * j + 8], T.dsc[:, 128 * j + 15:128 * j + 128:16], CORB, None, ADD, None, 8, "CORB dsc" + c, "obz" + c)
+            act(T.dab[:, u], pb[5][:, 128 * j:128 * j + 64], ACT.Abs, U, "NCEN bz" + c, "dab" + c, 5, bias=NCEN)
+        DAB, VAL, BZ = keys("dab", NCH), keys("val", NCH), keys("bz", NCH)
+        act(T.sg[:], T.dab[:], ACT.Sign, 256, DAB, "sg", bias=256.0, scale=-1.0)
+        act(T.ind[:], T.sg[:], ACT.Relu, 256, "sg", "ind")
+        act(T.fac[:], T.sg[:], ACT.Identity, 256, "sg", "fac", bias=(1 + INVB) / 2, scale=-(1 - INVB) / 2)
+        scan(pb[5][:, 0:256], T.fac[:], T.zero[:], 1.0, MUL, ADD, 256, "fac zero", "bz0 bz1", 5)
+        scan(pb[5][:, 256:512], T.ind[:], T.zero[:], 0.0, ADD, ADD, 256, "ind zero", "bz2 bz3", 5)
+        tt(T.wsel[:], T.ind[:], pb[5][:, 0:256], MUL, 256, "ind bz0 bz1", "wsel", 5)
+        tt(T.csel[:], T.ind[:], pb[5][:, 256:512], MUL, 256, "ind bz2 bz3", "csel", 5)
+        mm(group(pb[7][:, 0:256], [(T.dm[:], T.ind[:]), (T.j9[:], T.csel[:])], 256), "dm j9 ind csel", "b7", 7)
+        scan(T.ssc[:], T.rd[:], pb[7][:, 0:256], 0.0, ADD, MIN, 256, "b7 rd", "ssc", 7)
+        ts(T.slot[:], T.ssc[:, 15::16], CORS, None, ADD, None, 16, "ssc CORS", "slot")
+        mm([(pb[7][:, 256 + 8 * h:264 + 8 * h], T.val[:, 0, 128 * h:128 * h + 128], T.gsel[:], True, True, 8) for h in range(2)],
+           VAL + "gsel", "bt", 7)
+        ts(T.bti[:], pb[7][:, 256:272], -14 * SH, None, ADD, None, 16, "bt", "bti", 7)
+        ts(T.btm[:, 0:16], T.bti[:], 0x1E0F, None, ALU.bitwise_and, None, 16, "bti", "btm0")
+        ts(T.btm[:, 16:32], T.bti[:], 0x1F0, None, ALU.bitwise_and, None, 16, "bti", "btm1")
+        cp(T.btf[:], T.btm[:], 32, "btm0 btm1", "btf")
+        mm([(pb[7][:, 272 + 8 * h:280 + 8 * h], T.wsel[:, 128 * h:128 * h + 128], T.gsel[:], True, True, 8) for h in range(2)],
+           "wsel gsel", "wtp", 7)
+        act(T.wtt[:], pb[7][:, 272:288], ACT.Copy, 16, "wtp", "wtt", 7)
+        OH, OL = blocks(T.ohh, 128, 16), blocks(T.ohl, 32, 16)
+        for i in range(16):
+            ts(OH[i], T.chi[:], T.btf[:, i:i + 1], None, EQ, None, 128, "chi btf", "ohh%d" % i, f=0.5)
+            ts(OL[i], T.clo[:], T.btf[:, 16 + i:17 + i], T.wtt[:, i:i + 1], EQ, MUL, 32, "clo btf wtt", "ohl%d" % i, f=0.5)
+        tab = [(pb[5][:, 0:288:9], OH[0], OL[0], True, True, 32)]
+        for q in range(8):
+            tab += group(pb[5][:, 8 - q:288:9], [(OH[i], OL[i]) for i in (q, 8 + q)], 32)
+        mm(tab, keys("ohh", 16) + keys("ohl", 16), BZ, 5)
+        act(T.lg[:], pb[5][:, 0:288], ACT.Ln, 288, BZ, "lg", 5, bias=2.0 ** -63, scale=math.exp(0.69 * LNB), extra=1300.0 * (t == 0))
+        act(T.rr[:], T.lg[:], ACT.Identity, 288, "lg", "rr", bias=MAGIC, scale=-1.0 / LNB)
+        ts(T.kp[:], T.rr[:], -MAGIC, 48.0, ADD, MIN, 288, "rr", "kp")
+        act(T.ke[:], T.kp[:], ACT.Relu, 288, "kp", "ke", bias=-47.0)
+        act(T.kp[:, 0::9], T.fb[:], ACT.Copy, 32, "fb", "kp")
+        act(T.ke[:, 0::9], T.zero[:, 0:32], ACT.Copy, 32, "zero", "ke")
+        scan(T.ks[:], T.ke[:], T.kp[:], 0.0, MUL, ADD, 288, "ke kp", "ks")
+        ts(T.t2[:], T.ks[:, 8::9], A48, 384.0, ALU.is_lt, MUL, 32, "ks A48", "t2")
+        tt(T.t3[:], T.ks[:, 8::9], T.t2[:], ADD, 32, "ks t2", "t3")
+        ts(T.key[:], T.t3[:], N48, None, ADD, None, 32, "t3 N48", "key")
+        for j in range(NCH):
+            u = slice(U * j, U * j + U)
+            c = "%d " % j
+            hs, ks = halves(j)
+            ob, obz = T.obz[:, 8 * j:8 * j + 4], T.obz[:, 8 * j:8 * j + 8]
+            xb, xz = T.xbz[:, 128 * j:128 * j + 64], T.xbz[:, 128 * j + 64:128 * j + 128]
+            blk, fr = T.blk[:, u], T.fr[:, u]
+            cp(T.e16[:, u], swin.indirect(ob), U, SW + "obz" + c, "e16" + c, f=GA)
+            mm(sum([group(pb[4][:, 320 + 32 * h:352 + 32 * h], [(PM[2 * h + e], T.e16[:, U * j + e:U * j + U:2]) for e in range(2)], 32)
+                    for h in range(2)], []), keys("pm", 4) + "e16" + c, "eop", 4)
+            ts(T.eo[:, u], pb[4][:, 320:384], SH, None, ADD, None, U, "eop", "eo" + c, 4)
+            act(T.xbz[:, 128 * j:128 * j + 128], xwin.indirect(obz), ACT.Copy, 128, XW + "obz" + c, "xbz" + c, f=GA)
+            for h in (1, 0):
+                act(T.gx[:, hs[h]], xwin.indirect(T.eo[:, U * j + 32 * h:U * j + 32 * h + 32]), ACT.Copy, 512, XW + "eo" + c, "gx%d%d" % (j, h), f=GA)
+            ts(T.dead[:, u], T.e16[:, u], SH, 2.0, EQ, MUL, U, "e16" + c, "dead" + c, f=0.5)
+            mm(group(pb[4][:, 384:448], [(I, xb), (T.ineg[:], xz)], U), "ii ineg xbz" + c, "zbp", 4)
+            act(T.mzb[:, u], pb[4][:, 384:448], ACT.Abs, U, "zbp", "mzb" + c, 4)
+            for i, (xx, out, name) in enumerate(((xz, T.az, "az"), (xb, T.ab, "ab"))):
+                b, d = (3, 2) if j < 2 or i == 0 else (1, 0)
+                mm([(pb[b][:, k::8], I, xx, True, True, U) for k in range(8)], "ii xbz" + c, "b%d" % b, b)
+                tt(out[:, hs[1]], T.gx[:, hs[1]], pb[b][:], MAX, 512, "gx%d1 b%d" % (j, b), "%s%d1" % (name, j), b)
+                mm([(pb[d][:], T.ineg[:], T.gx[:, hs[0]], True, False, 512)] + [(pb[d][:, k::8], I, xx, False, k == 7, U) for k in range(8)],
+                   "ii ineg gx%d0 xbz%d" % (j, j), "b%d" % d, d)
+                act(out[:, hs[0]], pb[d][:], ACT.Abs, 512, "b%d" % d, "%s%d0" % (name, j), d)
+            mm(group(pb[6][:, 128:192], [(T.jj[:], T.mzb[:, u])] + [(R[k], T.gx[:, ks[k]]) for k in range(8, 16)], U),
+               "wd jj gx%d1 mzb%d" % (j, j), "accs", 6)
+            mm(group(pb[6][:, 0:64], [(T.jhi[:], xz)] + [(R2[k], T.az[:, ks[k]]) for k in range(16)], U),
+               "wd wd2 jhi az%d0 az%d1 xbz%d" % (j, j, j), "acce", 6)
+            act(T.ae[:, u], pb[6][:, 0:64], ACT.Copy, U, "acce", "ae" + c, 6)
+            tt(blk, T.ae[:, u], pb[6][:, 128:192], ALU.is_lt, U, "accs ae" + c, "blk" + c, 6)
+            mm(group(pb[6][:, 64:128], [(T.jhi[:], xb), (T.ibig[:], T.dead[:, u])] + [(R2[k], T.ab[:, ks[k]]) for k in range(16)], U),
+               "wd wd2 jhi ibig ab%d0 ab%d1 xbz%d dead%d" % (j, j, j, j), "accb", 6)
+            tt(fr, T.ae[:, u], pb[6][:, 64:128], ALU.is_lt, U, "accb ae" + c, "fr" + c, 6)
+            mm(group(pb[6][:, 192:256], [(CK[0], ONE), (T.jnbig[:], blk), (T.ibig[:], fr)], U)
+               + group(pb[6][:, 256:320], [(CK[1], ONE), (T.jj[:], T.val[:, 1, u]), (T.jj[:], T.val[:, 2, u]), (T.jbig[:], blk), (LIS[0], fr)], U),
+               "ck0 ck1 ones jnbig jbig ibig li0 jj val%d blk%d fr%d" % (j, j, j), "p12", 6)
+            tt(T.keep[:, u], T.e16[:, u], pb[6][:, 192:256], MAX, U, "p12 e16" + c, "keep" + c, 6)
+            tt(T.nn[:, u], T.keep[:, u], pb[6][:, 256:320], MIN, U, "p12 keep" + c, "nn" + c, 6)
+            cp(T.ns[:, 0:2320].indirect(T.slot[:, 4 * j:4 * j + 4]), T.nn[:, u], U, "slot nn" + c, "ns", f=SC)
+        cp(T.cv[:], T.ns[:, 0:432], 432, "ns", "cv")
+        mm([(pb[7][:, 48 * d:48 * d + 48], T.ii[:, 16 * d:16 * d + 128], T.cv[:, d::9], True, True, 48) for d in range(8)],
+           "cv ii", "b7 bt wtp", 7)
+        act(nw[t][:, 0:384], pb[7][:, 0:384], ACT.Copy, 384, "b7 bt wtp", "nwn%d" % t, 7)
+        cp(nat[t + 1][:], nw[t][:, 0:896].indirect(T.key[:]), 512, "nwn%d nwo%d key" % (t, t), "nat%d" % (t + 1), f=GA)
+        if t == 0:
+            act(T.nw1[:, 384:896], T.nw0[:, 0:896].indirect(T.key[:]), ACT.Copy, 512, "nwn0 nwo0 key", "nwo1", f=GA)
+    mm([(pb[0][:, j::4], T.nat2[:, 128 * j:128 * j + 128], I, True, True, 128) for j in range(4)], "nat2 ii", "b0", 0)
+    cp(T.pz[:], pb[0][:], 512, "b0", "pz", 0)
+    op("g", 1000.0, "pz", "sent2", send(T.pz, T.hz, T.lz, 64, T.sem.h2, T.sem.arr2), done=())
+    cp(T.lz[:, rank * 64:(rank + 1) * 64], T.pz[:, rank * 64:(rank + 1) * 64], 64, "pz", "lzown", f=0.5)
+    op(None, 5000.0, "sent2", "lz", None, done=("arr2", n_arr))
+    for h in range(2):
+        mm([(pb[1 + h][:, 128 * j:128 * j + 128], T.lz[:, 2 * h + j::4], I, True, True, 128) for j in range(2)], "lz lzown ii", "b%d" % (1 + h), 1 + h)
+    ts(T.yo[:, 0:256], pb[1][:, 0:256], SH, None, ADD, None, 256, "b1", "yo0", 1)
+    op("s", 60.0, "yo0", "", lambda: g.sync.dma_start(T.y[:, 0:256], T.yo[:, 0:256]).then_inc(T.sem.st0, 16), done=("st0", 16), lag=2000.0)
+    act(T.yo[:, 256:512], pb[2][:, 0:256], ACT.Identity, 256, "b2", "yo1", 2, bias=SH)
+    op("a", 60.0, "yo1", "", lambda: g.scalar.dma_start(T.y[:, 256:512], T.yo[:, 256:512]).then_inc(T.sem.st1, 16), done=("st1", 16), lag=2000.0)
+    return ops, 2 * n_sent
+
+
+def schedule(ops, bump, slack=60.0):
+    n = len(ops)
+    succ = [[] for _ in range(n)]
+    for i, o in enumerate(ops):
+        for d in o["deps"]:
+            succ[d].append(i)
+    prio = [0.0] * n
+    for i in range(n - 1, -1, -1):
+        prio[i] = ops[i]["cost"] + ops[i]["lag"] + max([prio[s] + LAT for s in succ[i]] + [0.0])
+    prio = [a + b for a, b in zip(prio, bump)]
+    left = [len(o["deps"]) for o in ops]
+    ready = [i for i in range(n) if left[i] == 0]
+    end, start, dep_t = [0.0] * n, [0.0] * n, [0.0] * n
+    free, users, order = {}, {}, []
+    extra = [set() for _ in range(n)]
+
+    def est(i):
+        o = ops[i]
+        t = max(dep_t[i], free.get(o["eng"], 0.0))
+        for e, k in users.get(o["bank"], {}).items():
+            if e != o["eng"]:
+                t = max(t, end[k] + LAT)
+        return t
+    while ready:
+        es = {i: est(i) for i in ready}
+        first = min(ready, key=lambda i: (es[i], -prio[i]))
+        eng = ops[first]["eng"]
+        i = max([k for k in ready if ops[k]["eng"] == eng and es[k] <= es[first] + slack], key=lambda k: prio[k])
+        o = ops[i]
+        start[i] = es[i]
+        end[i] = es[i] + o["cost"] + o["lag"]
+        if eng:
+            free[eng] = es[i] + o["cost"]
+        if o["bank"] is not None:
+            us = users.setdefault(o["bank"], {})
+            extra[i].update(k for e, k in us.items() if e != eng)
+            us[eng] = i
+        ready.remove(i)
+        order.append(i)
+        for s in succ[i]:
+            left[s] -= 1
+            dep_t[s] = max(dep_t[s], end[i] + LAT)
+            if left[s] == 0:
+                ready.append(s)
+    return order, extra, start, end
+
+
+def best_schedule(ops, tries=3000):
+    n = len(ops)
+    seed = [7]
+
+    def rnd(m):
+        seed[0] = (seed[0] * 1103515245 + 12345) % 2147483648
+        return (seed[0] >> 8) % m
+    bump = [3000.0 if o["cost"] < 420 else 0.0 for o in ops]
+    best = schedule(ops, bump)
+    keep = best
+    for _ in range(tries):
+        b = list(bump)
+        for _k in range((1, 2, 4)[rnd(3)]):
+            i, w, d = rnd(n), (1, 1, 3, 8, 20)[rnd(5)], (rnd(2001) - 1000) * (1.0, 3.0, 8.0)[rnd(3)]
+            for x in range(i, min(n, i + w)):
+                b[x] += d
+        r = schedule(ops, b)
+        if max(r[3]) <= max(best[3]) + 30.0:
+            best, bump = r, b
+            if max(r[3]) < max(keep[3]):
+                keep = r
+    return keep
+
+
+CACHE = {}
+
+
+def rank_program(g, core, T, topo):
+    rank = T.rank_of(core)
+    if rank is None:
+        for r, (direct, via) in enumerate(routes(T, topo)):
+            for i, (h, rs) in enumerate(via):
+                if h == core:
+                    helper_program(g, core, T, topo, r, rs, len(engine_plan(T, topo, r, direct, via)[1][i]))
+        return
+    ops, n_sent = build(g, core, T, topo, rank)
+    if "s" not in CACHE:
+        CACHE["s"] = best_schedule(ops)
+    order, extra = CACHE["s"][0:2]
+    queue = {"v": g.vector, "a": g.scalar, "p": g.tensor, "g": g, "s": g.sync}
+    count = {k: 0 for k in QSEM}
+    waited = {k: {} for k in queue}
+    done = {}
+    for i in order:
+        o = ops[i]
+        eng = o["eng"]
+        if eng is None:
+            done[i] = o["done"]
+            continue
+        need = {}
+        for d in set(o["deps"]) | extra[i]:
+            if not done[d] or (eng == "p" and ops[d]["eng"] == "p"):
+                continue
+            s, v = done[d]
+            need[s] = max(need.get(s, 0), v)
+        for s, v in sorted(need.items()):
+            if waited[eng].get(s, 0) < v:
+                queue[eng].wait_ge(T.sem[s], v)
+                waited[eng][s] = v
+        ins = o["fn"]()
+        if o["done"] is None:
+            count[eng] += 1
+            ins.then_inc(T.sem[QSEM[eng]], 1)
+            done[i] = (QSEM[eng], count[eng])
+        else:
+            done[i] = o["done"]
+    for k, s in QSEM.items():
+        g.wait_ge(T.sem[s], count[k])
+    g.wait_ge(T.sem.sent, n_sent)
+    g.wait_ge(T.sem.st0, 16)
+    g.wait_ge(T.sem.st1, 16)

@@ -16,24 +16,27 @@ FAR = 1024.0
 SCRATCH = {}
 for _d, _l in (
     ("int32", "sin 512 pi 16 pj 16 pk 8 ti 160 bti 16 btm 32"),
-    ("float16", "s16 512 pa 1024 la 1024 ha 256 pz 512 lz 512 hz 128 nat0 512 nat1 512 nat2 512 cv 432 wn 512 e16 256"),
+    ("float16", "s16 512 pa 512 la 512 ha 128 pz 512 lz 512 hz 128 nat0 512 nat1 512 nat2 512 cv 432 wn 512 e16 256"),
     ("uint16", "off 256 obz 32 eo 256 slot 16 key 32 chi 128 clo 32"),
-    ("float32", "yo 512 sw 4104 nw0 896 nw1 896 dsc 512 gs 4096 ae 256 keep 256 nn 256 ns 2320 dab 256 ssc 256 btf 32 "
-                "wtt 16 lg 288 rr 288 kp 288 ke 288 ks 288 t2 32 t3 32 mf 144 mhi 128 mlo 272 pc 16 plc 16 kmask 16 gmask 8 "
+    ("float32", "yo 512 sw 4488 dsc 512 gs 4096 ae 256 keep 256 nn 256 ns 2320 dab 256 ssc 256 btf 32 "
+                "wtt 16 lg 288 rr 288 kp 288 ke 288 ks 288 t2 32 t3 32 mf 144 mhi 128 mlo 144 pc 16 plc 16 kmask 16 gmask 8 "
                 "rd 256 fb 32 tf 256"),
-    ("bfloat16", "xin 512 xnat 512 xw 4112 ni 256 za 256 zb 256 dead 256 xbz 512 mzb 256 blk 256 fr 256 ind 256 fac 256 "
+    ("bfloat16", "xw 4112 ni 256 za 256 zb 256 dead 256 xbz 512 mzb 256 blk 256 fr 256 ind 256 fac 256 "
                  "wsel 256 csel 256 ohh 2048 ohl 512 ii 256 ineg 128 ibig 128 jj 128 sg 256 jhi 128 j9 128 jbig 128 "
-                 "jnbig 128 dm 128 shm 128 ish 128 km 256 tmpb 128 lt 256 li 256 wd 144 wd2 144 sel 2048 rep 1024 gsel 8 "
-                 "gx 4096 eqw 4096 eqc 4096 az 4096 ab 4096 pm 512 ck 384 ones 256 zero 256"),
+                 "jnbig 128 dm 128 shm 128 ish 128 km 128 tmpb 128 lt 256 li 256 wd 144 wd2 144 sel 2048 rep 1024 gsel 8 "
+                 "gx 4096 eqw 4096 eqc 4096 az 4096 ab 4096 pm 512 ck 384 ones 128 zero 256"),
 ):
     _w = _l.split()
     for _i in range(0, len(_w), 2):
         SCRATCH[_w[_i]] = ("sbuf", [128, int(_w[_i + 1])], _d)
 SCRATCH["val"] = ("sbuf", [128, 3, 256], "float16")
 SCRATCH["dx"] = ("dram", [16, 4096], "bfloat16")
+SCRATCH["xs"] = ("dram", [8, 128, 64], "bfloat16")
+SCRATCH["xl"] = ("dram", [8, 128, 64], "bfloat16")
+SCRATCH["xh"] = ("dram", [2, 128, 64], "bfloat16")
 for _b in range(8):
     SCRATCH["pb%d" % _b] = ("psum", [128, 512], "float32")
-SEMAPHORES = ["qv", "qa", "qp", "qg", "lds", "ldx", "arr1", "arr2", "h1", "h2", "sent", "st0", "st1", "dx1", "dx2"]
+SEMAPHORES = ["qv", "qa", "qp", "qg", "lds", "ldx", "arr0", "arr1", "arr2", "h0", "h1", "h2", "sent", "st0", "st1", "dx1", "dx2"]
 QSEM = {"v": "qv", "a": "qa", "p": "qp", "g": "qg"}
 LAT = 110.0
 
@@ -70,9 +73,13 @@ def engine_plan(T, topo, rank, direct, via):
     on = [e for e in topo.engines(c, via[0][0]) if e not in off]
     n, m = len(off) // len(far), len(on) // len(via)
     plan = {r: off[i * n:(i + 1) * n] for i, r in enumerate(far)}
+    xplan = dict(plan)
     for r in near:
         plan[r] = on[:m]
-    return plan, [on[i * m:(i + 1) * m] for i in range(len(via))]
+        xplan[r] = on[0:1]
+    (a, b), (d, e) = via[0][1], via[1][1]
+    xplan.update({a: on[1:2], b: on[2:4], d: on[4:6], e: on[6:8]})
+    return plan, [on[i * m:(i + 1) * m] for i in range(len(via))], xplan
 
 
 def helper_engines(T, topo, h, rs):
@@ -86,14 +93,16 @@ def dst(topo, d, s):
     return DstId(rid=rid, pnc=pid)
 
 
-def helper_program(g, core, T, topo, rank, rs, n_in):
+def helper_program(g, core, T, topo, rank, rs, n_in, n_x):
     es = helper_engines(T, topo, core, rs)
-    for land, to, w, arr, h in ((T.ha, T.la, 128, T.sem.arr1, T.sem.h1), (T.hz, T.lz, 64, T.sem.arr2, T.sem.h2)):
-        g.wait_ge(h, n_in)
+    here = slice(rank * 64, rank * 64 + 64)
+    for src, to, arr, h, n in (([T.xh[0], T.xh[1]], T.xl[rank], T.sem.arr0, T.sem.h0, n_x),
+                               ([T.ha[:, 0:64], T.ha[:, 64:128]], T.la[:, here], T.sem.arr1, T.sem.h1, n_in),
+                               ([T.hz[:, 0:64], T.hz[:, 64:128]], T.lz[:, here], T.sem.arr2, T.sem.h2, n_in)):
+        g.wait_ge(h, n)
         g.remote_dma_fused([RemoteDMATransfer(dst_ids=[dst(topo, T.cores[r], core)], dma_engine_mask=bits(es[i]), remote_sem=arr,
-                                              src=land[:, i * w:(i + 1) * w], dst=to[:, rank * w:(rank + 1) * w])
-                            for i, r in enumerate(rs)], local_sem=T.sem.sent)
-    g.wait_ge(T.sem.sent, 2 * sum(len(e) for e in es))
+                                              src=src[i], dst=to) for i, r in enumerate(rs)], local_sem=T.sem.sent)
+    g.wait_ge(T.sem.sent, 3 * sum(len(e) for e in es))
 
 
 def build(g, core, T, topo, rank):
@@ -101,17 +110,20 @@ def build(g, core, T, topo, rank):
     state = {}
     rts = routes(T, topo)
     direct, via = rts[rank]
-    plan, hplan = engine_plan(T, topo, rank, direct, via)
-    n_arr = 0
+    plan, hplan, xplan = engine_plan(T, topo, rank, direct, via)
+    n_arr = n_arx = 0
     for s in range(N):
         if s == rank:
             continue
         ds, vs = rts[s]
         if rank in ds:
-            n_arr += len(engine_plan(T, topo, s, ds, vs)[0][rank])
+            p = engine_plan(T, topo, s, ds, vs)
+            n_arr += len(p[0][rank])
+            n_arx += len(p[2][rank])
         else:
             h, rs = [e for e in vs if rank in e[1]][0]
             n_arr += len(helper_engines(T, topo, h, rs)[rs.index(rank)])
+            n_arx += len(helper_engines(T, topo, h, rs)[rs.index(rank)])
     pb = [T["pb%d" % b] for b in range(8)]
 
     def op(eng, cost, rd, wr, fn, bank=None, done=None, lag=0.0):
@@ -182,34 +194,41 @@ def build(g, core, T, topo, rank):
 
     GA, SC = 1.56, 3.8
     ADD, SUB, MUL, MAX, MIN, EQ = ALU.add, ALU.subtract, ALU.mult, ALU.max, ALU.min, ALU.is_equal
+    here = slice(rank * 64, rank * 64 + 64)
     op("s", 60.0, "", "sin", lambda: g.sync.dma_start(T.sin[:], T.stars[:]).then_inc(T.sem.lds, 16), done=("lds", 16), lag=2200.0)
-    op("a", 60.0, "", "xin", lambda: g.scalar.dma_start(T.xin[:], T.x[:]).then_inc(T.sem.ldx, 16), done=("ldx", 16), lag=2000.0)
-    ms(T.ones[:], 1.0, 128, "ones")
-    asel(T.ii[:], T.ones[:], [[0, 2], [-1, 128]], EQ, 0.0, 0, 1, 256, "ones", "ii")
+    op("a", 60.0, "", "xs", lambda: g.scalar.dma_start(T.xs[:], T.x[:]).then_inc(T.sem.ldx, 16), done=("ldx", 16), lag=2000.0)
+    ms(T.ones[:], 1.0, 64, "ones")
     I = T.ii[:, 0:128]
-    ts(T.s16[:], T.sin[:], -SH, None, ADD, None, 512, "sin", "s16")
-    mm([(pb[0][:, j::4], T.s16[:, 128 * j:128 * j + 128], I, True, True, 128) for j in range(4)], "s16 ii", "b0", 0)
-    mm([(pb[1][:, j::4], T.xin[:, 128 * j:128 * j + 128], I, True, True, 128) for j in range(4)], "xin ii", "b1", 1)
-    cp(T.pa[:, 1::2], pb[1][:], 512, "b1", "pa1", 1)
-    cp(T.pa[:, 0::2], pb[0][:], 512, "b0", "pa0", 0)
-
-    def send(src, land, to, w, hsem, arr):
-        def fn():
-            g.remote_dma_fused([RemoteDMATransfer(dst_ids=[dst(topo, h, core)], dma_engine_mask=bits(hplan[i]), remote_sem=hsem,
-                                                  src=src[:, rs[0] * w:(rs[0] + 2) * w], dst=land[:])
-                                for i, (h, rs) in enumerate(via)], local_sem=T.sem.sent)
-            g.remote_dma_fused([RemoteDMATransfer(dst_ids=[dst(topo, T.cores[r], core)], dma_engine_mask=bits(plan[r]), remote_sem=arr,
-                                                  src=src[:, r * w:(r + 1) * w], dst=to[:, rank * w:(rank + 1) * w])
-                                for r in direct], local_sem=T.sem.sent)
-        return fn
-    n_sent = sum(len(e) for e in hplan) + sum(len(plan[r]) for r in direct)
-    op("g", 1000.0, "pa0 pa1", "sent1", send(T.pa, T.ha, T.la, 128, T.sem.h1, T.sem.arr1), done=())
-    cp(T.la[:, rank * 128:(rank + 1) * 128], T.pa[:, rank * 128:(rank + 1) * 128], 128, "pa0 pa1", "laown", f=0.5)
-    op(None, 6000.0, "sent1", "la", None, done=("arr1", n_arr))
+    asel(I, T.ones[:], [[-1, 128]], EQ, 0.0, 0, 1, 128, "ones", "ii")
     op("g", 170.0, "", "pi", lambda: g.iota(T.pi[:], [[1, 16]], 0, 1))
-    iota(T.mlo[:], [[0, 17], [1, 16]], 272, "", "mlo")
+    iota(T.mlo[:], [[0, 9], [1, 16]], 144, "", "mlo")
     iota(T.mhi[:], [[1, 8], [0, 16]], 128, "", "mhi")
     iota(T.mf[:], [[1, 144]], 144, "", "mf")
+
+    def send_x():
+        g.remote_dma_fused([RemoteDMATransfer(dst_ids=[dst(topo, h, core)], dma_engine_mask=bits(xplan[r]), remote_sem=T.sem.h0,
+                                              src=T.xs[r], dst=T.xh[i]) for h, rs in via for i, r in enumerate(rs)]
+                           + [RemoteDMATransfer(dst_ids=[dst(topo, T.cores[r], core)], dma_engine_mask=bits(xplan[r]), remote_sem=T.sem.arr0,
+                                                src=T.xs[r], dst=T.xl[rank]) for r in direct], local_sem=T.sem.sent)
+    op("g", 1000.0, "xs ii pi mlo mhi mf", "sent0", send_x, done=())
+    op(None, 6000.0, "sent0", "xl", None, done=("arr0", n_arx))
+    ts(T.s16[:], T.sin[:], -SH, None, ADD, None, 512, "sin", "s16")
+    mm([(pb[0][:, j::4], T.s16[:, 128 * j:128 * j + 128], I, True, True, 128) for j in range(4)], "s16 ii", "b0", 0)
+    cp(T.pa[:], pb[0][:], 512, "b0", "pa", 0)
+
+    def send(src, land, to, hsem, arr):
+        def fn():
+            g.remote_dma_fused([RemoteDMATransfer(dst_ids=[dst(topo, h, core)], dma_engine_mask=bits(hplan[i]), remote_sem=hsem,
+                                                  src=src[:, rs[0] * 64:(rs[0] + 2) * 64], dst=land[:])
+                                for i, (h, rs) in enumerate(via)], local_sem=T.sem.sent)
+            g.remote_dma_fused([RemoteDMATransfer(dst_ids=[dst(topo, T.cores[r], core)], dma_engine_mask=bits(plan[r]), remote_sem=arr,
+                                                  src=src[:, r * 64:(r + 1) * 64], dst=to[:, here])
+                                for r in direct], local_sem=T.sem.sent)
+        return fn
+    n_sent = 2 * (sum(len(e) for e in hplan) + sum(len(plan[r]) for r in direct)) + sum(len(e) for e in xplan.values())
+    op("g", 1000.0, "pa sent0", "sent1", send(T.pa, T.ha, T.la, T.sem.h1, T.sem.arr1), done=())
+    cp(T.la[:, here], T.pa[:, here], 64, "pa", "laown", f=0.5)
+    op(None, 5000.0, "sent1", "la", None, done=("arr1", n_arr))
     P, PHI, CORB, CORS, NCEN, DV, A48, N48, WQ, WDC, W0, FB0, DV0 = blocks(T.pc, 1, 13)
     PLO, ORD1 = T.plc[:, 0:1], T.plc[:, 11:12]
     cp(P, T.pi[:, 0:1], 1, "pi", "P")
@@ -217,16 +236,17 @@ def build(g, core, T, topo, rank):
     cp(T.plc[:], T.pj[:], 16, "pj", "plc")
     ts(PHI, P, PLO, 0.0625, SUB, MUL, 1, "P plc", "PHI")
     ts(T.jj[:], T.mhi[:], PHI, None, EQ, None, 128, "mhi PHI", "jj")
-    ts(T.km[:], T.mlo[:, 0:256], PLO, None, EQ, None, 256, "mlo plc", "km")
+    ts(T.km[:], T.mlo[:, 0:128], PLO, None, EQ, None, 128, "mlo plc", "km")
     ts(T.gmask[:], T.mf[:, 0:8], PHI, None, EQ, None, 8, "mf PHI", "gmask")
     ts(T.kmask[:], T.mf[:, 0:16], PLO, None, EQ, None, 16, "mf plc", "kmask")
     cp(T.gsel[:], T.gmask[:], 8, "gmask", "gsel")
     REP, SEL, PM, CK = blocks(T.rep, 128, 8), blocks(T.sel, 128, 16), blocks(T.pm, 128, 4), blocks(T.ck, 128, 3)
     LTS, LIS = blocks(T.lt, 128, 2), blocks(T.li, 128, 2)
     for r in range(8):
-        act(REP[r], T.km[:, 0:128], ACT.Copy, 128, "km gmask", "rep%d" % r, scale=T.gmask[:, r:r + 1])
+        act(REP[r], T.km[:], ACT.Copy, 128, "km gmask", "rep%d" % r, scale=T.gmask[:, r:r + 1])
     for k in range(16):
         ts(SEL[k], T.jj[:], T.kmask[:, k:k + 1], None, MUL, None, 128, "jj kmask", "sel%d" % k, f=0.5)
+    act(T.ii[:, 128:256], I, ACT.Copy, 128, "ii", "ii2")
     for name, src, c in (("ineg", "ii", -1.0), ("ibig", "ii", 4096.0), ("j9", "jj", 9.0), ("jbig", "jj", 4096.0), ("jnbig", "jj", -4096.0)):
         act(T[name][:], T[src][:, 0:128], ACT.Copy, 128, src, name, scale=c)
     for col, name, src, sn, a, b in ((CORS, "CORS", PLO, "plc", -BIG, 15 * BIG - 9.0), (CORB, "CORB", PLO, "plc", -BIG, 15 * BIG - 30 * SH),
@@ -234,7 +254,7 @@ def build(g, core, T, topo, rank):
                                      (N48, "N48", PHI, "PHI", -48.0, 0.0), (WDC, "WDC", PHI, "PHI", 16.0, 15.0),
                                      (W0, "W0", PHI, "PHI", 512.0, -SH)):
         ts(col, src, a, b, MUL, ADD, 1, sn, name)
-    ts(FB0, PHI, 48.0, PLO, MUL, ADD, 1, "PHI plc", "FB0")
+    ts(FB0, PHI, 560.0, PLO, MUL, ADD, 1, "PHI plc", "FB0")
     ts(T.pk[:, 0:1], PHI, PLO, 8.0, SUB, ADD, 1, "PHI plc", "pk0")
     ts(T.pk[:, 1:2], T.pk[:, 0:1], 7, None, ALU.bitwise_and, None, 1, "pk0", "pk1")
     cp(DV0, T.pk[:, 1:2], 1, "pk1", "DV0")
@@ -243,12 +263,13 @@ def build(g, core, T, topo, rank):
     act(T.dm[:], T.jj[:], ACT.Copy, 128, "jj DV", "dm", scale=DV)
     ts(T.wd[:], T.mf[:], WDC, None, EQ, None, 144, "mf WDC", "wd")
     act(T.wd2[:], T.wd[:], ACT.Copy, 144, "wd", "wd2", scale=2.0)
-    ts(T.rd[:], T.km[:], HUGE + BIG, -BIG, MUL, ADD, 256, "km", "rd")
+    for h in range(2):
+        act(T.rd[:, 128 * h:128 * h + 128], T.km[:], ACT.Identity, 128, "km", "rd%d" % h, scale=HUGE + BIG, bias=-BIG)
     act(T.fb[:], T.mf[:, 0:32], ACT.Identity, 32, "mf FB0", "fb", scale=16.0, bias=FB0)
     ts(T.tmpb[:], T.mlo[:, 0:128], 8.0, -1.0, ALU.is_ge, MUL, 128, "mlo", "tmpb")
     tt(T.jhi[:], T.tmpb[:], T.jj[:], MUL, 128, "tmpb jj", "jhi")
     for i in range(4):
-        asel(PM[i], T.ones[:, 0:128], [[-16, 8], [-256, 2], [-1, 8]], EQ, 0.0, 256 * (i % 2) - 8 * (i // 2), 1, 128, "ones sent1", "pm%d" % i)
+        asel(PM[i], T.ones[:], [[-16, 8], [-256, 2], [-1, 8]], EQ, 0.0, 256 * (i % 2) - 8 * (i // 2), 1, 128, "ones sent1", "pm%d" % i)
     iota(T.tf[:], [[2, 256]], 256, "sent1", "tf")
     asel(LTS[0], T.jbig[:], [[1, 128]], ALU.is_gt, 0.0, 0, -1, 128, "jbig sent1", "lt0")
     ts(T.tmpb[:], T.mlo[:, 11:139], ORD1, None, ALU.is_gt, None, 128, "mlo plc", "tmpb")
@@ -266,30 +287,26 @@ def build(g, core, T, topo, rank):
     for i, c in enumerate((-16.0, -464.0, 256.0)):
         ms(CK[i], c, 64, "ck%d" % i)
     ms(T.zero[:], 0.0, 128, "zero")
-    ms(T.sw[:, 4096:4104], SH, 8, "sw8")
+    ms(T.sw[:, 4480:4488], SH, 8, "sw8")
     ms(T.xw[:, 4096:4112], FAR, 16, "xw8")
     ms(T.ns[:, 0:432], 0.0, 432, "ns")
     ONE = T.ones[:, 0:64]
     R = [T.wd[:, 15 - k:143 - k] for k in range(16)]
     R2 = R[0:8] + [T.wd2[:, 15 - k:143 - k] for k in range(8, 16)]
     SW, XW = keys("sw", 9), "xw xw8 "
-    swin, xwin = T.sw[:, 0:4104], T.xw[:, 0:4112]
+    swin, xwin = T.sw[:, 384:4488], T.xw[:, 0:4112]
     nat = [T.nat0, T.nat1, T.nat2]
-    nw = [T.nw0, T.nw1]
-    mm([(pb[0][:, 128 * j:128 * j + 128], T.la[:, 2 * j::8], I, True, True, 128) for j in range(4)], "la laown ii", "b0", 0)
+    mm([(pb[0][:, 128 * j:128 * j + 128], T.la[:, j::4], I, True, True, 128) for j in range(4)], "la laown ii", "b0", 0)
     cp(T.nat0[:], pb[0][:], 512, "b0", "nat0", 0)
-    mm([(pb[6][:, 128 * j:128 * j + 128], T.la[:, 2 * j + 1::8], I, True, True, 128) for j in range(4)], "la laown ii", "acce accb accs p12", 6)
-    act(T.xnat[:], pb[6][:], ACT.Copy, 512, "acce accb accs p12", "xnat", 6)
-    act(T.nw0[:, 384:896], pb[0][:], ACT.Copy, 512, "b0 nat0", "nwo0", 0)
 
     def x_out():
         for r in range(8):
-            g.sync.dma_start(T.dx[:, 512 * r:512 * r + 512], T.xnat[16 * r:16 * r + 16, :]).then_inc(T.sem.dx1, 16)
+            g.sync.dma_start(T.dx[:, 512 * r:512 * r + 512], T.xs[r] if r == rank else T.xl[r]).then_inc(T.sem.dx1, 16)
 
     def x_in():
         for r in range(8):
             g.sync.dma_start(T.xw[16 * r:16 * r + 16, 0:4096], T.dx[:]).then_inc(T.sem.dx2, 16)
-    op("s", 800.0, "xnat", "dx", x_out, done=("dx1", 128), lag=2500.0)
+    op("s", 800.0, "xs xl", "dx", x_out, done=("dx1", 128), lag=2500.0)
     op("s", 800.0, "dx", "xw", x_in, done=("dx2", 128), lag=7000.0)
 
     def halves(j):
@@ -301,12 +318,13 @@ def build(g, core, T, topo, rank):
         wk = "wn%d " % t
         LT, LI = LTS[t], LIS[t]
         for r in range(8):
-            b = [1, 2, 3][r % 3] if t == 0 else (r + 1) % 4
+            b = (r + 1) % 4
+            o = T.sw[:, 384 + 512 * r:896 + 512 * r]
             mm([(pb[b][:], REP[r], nat[t][:], True, True, 512)], nk + "rep%d" % r, "b%d" % b, b)
             if r % 2 == 0:
-                act(T.sw[:, 512 * r:512 * r + 512], pb[b][:], ACT.Copy, 512, "b%d" % b, "sw%d" % r, b)
+                act(o, pb[b][:], ACT.Copy, 512, "b%d" % b, "sw%d" % r, b)
             else:
-                cp(T.sw[:, 512 * r:512 * r + 512], pb[b][:], 512, "b%d" % b, "sw%d" % r, b)
+                cp(o, pb[b][:], 512, "b%d" % b, "sw%d" % r, b)
         mm(sum([group(pb[7][:, 128 * h:128 * h + 128], [(PM[2 * h + e], nat[t][:, t + 2 * e::4]) for e in range(2)], 128) for h in range(2)], []),
            keys("pm", 4) + nk, "b7", 7)
         ts(T.off[:], pb[7][:, 0:256], SH, None, ADD, None, 256, "b7", "off", 7)
@@ -344,7 +362,7 @@ def build(g, core, T, topo, rank):
             mm(group(pb[5][:, 128 * j:128 * j + 64], [(CK[2], ONE), (T.jj[:], T.val[:, 0, u])], U)
                + group(pb[5][:, 128 * j + 64:128 * j + 128], [(T.jj[:], T.val[:, 1, u]), (T.jj[:], T.val[:, 2, u])], U),
                "jj ck2 ones val" + c, "bz" + c, 5)
-            scan(T.dsc[:, 128 * j:128 * j + 128], T.rd[:, 0:128], pb[5][:, 128 * j:128 * j + 128], 0.0, ADD, MIN, 128, "rd bz" + c, "dsc" + c, 5)
+            scan(T.dsc[:, 128 * j:128 * j + 128], T.rd[:, 0:128], pb[5][:, 128 * j:128 * j + 128], 0.0, ADD, MIN, 128, "rd0 bz" + c, "dsc" + c, 5)
             ts(T.obz[:, 8 * j:8 * j + 8], T.dsc[:, 128 * j + 15:128 * j + 128:16], CORB, None, ADD, None, 8, "CORB dsc" + c, "obz" + c)
             act(T.dab[:, u], pb[5][:, 128 * j:128 * j + 64], ACT.Abs, U, "NCEN bz" + c, "dab" + c, 5, bias=NCEN)
         DAB, VAL, BZ = keys("dab", NCH), keys("val", NCH), keys("bz", NCH)
@@ -356,7 +374,7 @@ def build(g, core, T, topo, rank):
         tt(T.wsel[:], T.ind[:], pb[5][:, 0:256], MUL, 256, "ind bz0 bz1", "wsel", 5)
         tt(T.csel[:], T.ind[:], pb[5][:, 256:512], MUL, 256, "ind bz2 bz3", "csel", 5)
         mm(group(pb[7][:, 0:256], [(T.dm[:], T.ind[:]), (T.j9[:], T.csel[:])], 256), "dm j9 ind csel", "b7", 7)
-        scan(T.ssc[:], T.rd[:], pb[7][:, 0:256], 0.0, ADD, MIN, 256, "b7 rd", "ssc", 7)
+        scan(T.ssc[:], T.rd[:], pb[7][:, 0:256], 0.0, ADD, MIN, 256, "b7 rd0 rd1", "ssc", 7)
         ts(T.slot[:], T.ssc[:, 15::16], CORS, None, ADD, None, 16, "ssc CORS", "slot")
         mm([(pb[7][:, 256 + 8 * h:264 + 8 * h], T.val[:, 0, 128 * h:128 * h + 128], T.gsel[:], True, True, 8) for h in range(2)],
            VAL + "gsel", "bt", 7)
@@ -426,15 +444,13 @@ def build(g, core, T, topo, rank):
             cp(T.ns[:, 0:2320].indirect(T.slot[:, 4 * j:4 * j + 4]), T.nn[:, u], U, "slot nn" + c, "ns", f=SC)
         cp(T.cv[:], T.ns[:, 0:432], 432, "ns", "cv")
         mm([(pb[7][:, 48 * d:48 * d + 48], T.ii[:, 16 * d:16 * d + 128], T.cv[:, d::9], True, True, 48) for d in range(8)],
-           "cv ii", "b7 bt wtp", 7)
-        act(nw[t][:, 0:384], pb[7][:, 0:384], ACT.Copy, 384, "b7 bt wtp", "nwn%d" % t, 7)
-        cp(nat[t + 1][:], nw[t][:, 0:896].indirect(T.key[:]), 512, "nwn%d nwo%d key" % (t, t), "nat%d" % (t + 1), f=GA)
-        if t == 0:
-            act(T.nw1[:, 384:896], T.nw0[:, 0:896].indirect(T.key[:]), ACT.Copy, 512, "nwn0 nwo0 key", "nwo1", f=GA)
+           "cv ii ii2", "b7 bt wtp", 7)
+        act(T.sw[:, 0:384], pb[7][:, 0:384], ACT.Copy, 384, "b7 bt wtp", "nwn", 7)
+        cp(nat[t + 1][:], T.sw[:, 0:4488].indirect(T.key[:]), 512, SW + "nwn key", "nat%d" % (t + 1), f=GA)
     mm([(pb[0][:, j::4], T.nat2[:, 128 * j:128 * j + 128], I, True, True, 128) for j in range(4)], "nat2 ii", "b0", 0)
     cp(T.pz[:], pb[0][:], 512, "b0", "pz", 0)
-    op("g", 1000.0, "pz", "sent2", send(T.pz, T.hz, T.lz, 64, T.sem.h2, T.sem.arr2), done=())
-    cp(T.lz[:, rank * 64:(rank + 1) * 64], T.pz[:, rank * 64:(rank + 1) * 64], 64, "pz", "lzown", f=0.5)
+    op("g", 1000.0, "pz", "sent2", send(T.pz, T.hz, T.lz, T.sem.h2, T.sem.arr2), done=())
+    cp(T.lz[:, here], T.pz[:, here], 64, "pz", "lzown", f=0.5)
     op(None, 5000.0, "sent2", "lz", None, done=("arr2", n_arr))
     for h in range(2):
         mm([(pb[1 + h][:, 128 * j:128 * j + 128], T.lz[:, 2 * h + j::4], I, True, True, 128) for j in range(2)], "lz lzown ii", "b%d" % (1 + h), 1 + h)
@@ -442,7 +458,7 @@ def build(g, core, T, topo, rank):
     op("s", 60.0, "yo0", "", lambda: g.sync.dma_start(T.y[:, 0:256], T.yo[:, 0:256]).then_inc(T.sem.st0, 16), done=("st0", 16), lag=2000.0)
     act(T.yo[:, 256:512], pb[2][:, 0:256], ACT.Identity, 256, "b2", "yo1", 2, bias=SH)
     op("a", 60.0, "yo1", "", lambda: g.scalar.dma_start(T.y[:, 256:512], T.yo[:, 256:512]).then_inc(T.sem.st1, 16), done=("st1", 16), lag=2000.0)
-    return ops, 2 * n_sent
+    return ops, n_sent
 
 
 def schedule(ops, bump, slack=60.0):
@@ -492,7 +508,7 @@ def schedule(ops, bump, slack=60.0):
     return order, extra, start, end
 
 
-def best_schedule(ops, tries=3000):
+def best_schedule(ops, tries=5000):
     n = len(ops)
     seed = [7]
 
@@ -525,7 +541,8 @@ def rank_program(g, core, T, topo):
         for r, (direct, via) in enumerate(routes(T, topo)):
             for i, (h, rs) in enumerate(via):
                 if h == core:
-                    helper_program(g, core, T, topo, r, rs, len(engine_plan(T, topo, r, direct, via)[1][i]))
+                    p = engine_plan(T, topo, r, direct, via)
+                    helper_program(g, core, T, topo, r, rs, len(p[1][i]), sum(len(p[2][k]) for k in rs))
         return
     ops, n_sent = build(g, core, T, topo, rank)
     if "s" not in CACHE:

import math
from concourse.bass import DstId, RemoteDMATransfer
from concourse.mybir import AluOpType, ActivationFunctionType

ALU = AluOpType
ACT = ActivationFunctionType
N, W, RO = 8, 4096, 2
SH = 2048.0
NCH, U = 4, 64
BIG, HUGE = 65536.0, 4194304.0
INVB = 27.0 / 64.0
LNB = -math.log(INVB)
MAGIC = 12582912.0
FAR = 1024.0

SCRATCH = {}
for _d, _l in (
    ("int32", "sin 512 pi 16 pj 16 pk 8 ti 160 bti 16 btm 32"),
    ("float16", "s16 512 pa 512 la 512 ha 128 pz 512 lz 512 hz 128 nat0 512 nat1 512 nat2 512 cv 432 wn 512 e16 256"),
    ("uint16", "off 256 obz 32 eo 256 slot 16 key 32 chi 128 clo 32"),
    ("float32", "yo 512 sw 4488 dsc 512 gs 4096 ae 256 keep 256 nn 256 ns 2320 dab 256 ssc 256 btf 32 "
                "wtt 16 lg 288 rr 288 kp 288 ke 288 ks 288 t2 32 t3 32 mf 144 mhi 128 mlo 144 pc 16 plc 16 kmask 16 gmask 8 "
                "rd 256 fb 32 tf 256"),
    ("bfloat16", "xw 4112 ni 256 za 256 zb 256 dead 256 xbz 512 mzb 256 blk 256 fr 256 ind 256 fac 256 "
                 "wsel 256 csel 256 ohh 2048 ohl 512 ii 256 ineg 128 ibig 128 jj 128 sg 256 jhi 128 j9 128 jbig 128 "
                 "jnbig 128 dm 128 shm 128 ish 128 km 128 tmpb 128 lt 256 li 256 wd 144 wd2 144 sel 2048 rep 1024 gsel 8 "
                 "gx 4096 eqw 4096 eqc 4096 az 4096 ab 4096 pm 512 ck 384 ones 128 zero 256"),
):
    _w = _l.split()
    for _i in range(0, len(_w), 2):
        SCRATCH[_w[_i]] = ("sbuf", [128, int(_w[_i + 1])], _d)
SCRATCH["val"] = ("sbuf", [128, 3, 256], "float16")
SCRATCH["dx"] = ("dram", [16, 4096], "bfloat16")
SCRATCH["xs"] = ("dram", [8, 128, 64], "bfloat16")
SCRATCH["xl"] = ("dram", [8, 128, 64], "bfloat16")
SCRATCH["xh"] = ("dram", [2, 128, 64], "bfloat16")
for _b in range(8):
    SCRATCH["pb%d" % _b] = ("psum", [128, 512], "float32")
SEMAPHORES = ["qv", "qa", "qp", "qg", "lds", "ldx", "arr0", "arr1", "arr2", "h0", "h1", "h2", "sent", "st0", "st1", "dx1", "dx2"]
QSEM = {"v": "qv", "a": "qa", "p": "qp", "g": "qg"}
LAT = 110.0


def routes(T, topo):
    out = []
    for c in T.cores:
        direct = [r for r, d in enumerate(T.cores) if d != c and topo.may_write(c, d)]
        rest = [r for r, d in enumerate(T.cores) if d != c and not topo.may_write(c, d)]
        sets = {}
        for r in rest:
            sets.setdefault((topo.host(T.cores[r]), topo.chip(T.cores[r])), []).append(r)
        hs = [h for h in topo.cores_of(c) if T.rank_of(h) is None and topo.die(h) == topo.die(c)
              and all(topo.may_write(h, T.cores[r]) for r in rest)]
        via = [(hs[i], rs) for i, rs in enumerate(sets.values())]
        for h, rs in via:
            assert rs == list(range(rs[0], rs[0] + 2))
        out.append((direct, via))
    return out


def bits(es):
    m = 0
    for e in es:
        m |= 1 << e
    return m


def engine_plan(T, topo, rank, direct, via):
    c = T.cores[rank]
    far = [r for r in direct if topo.same_plane(c, T.cores[r])]
    near = [r for r in direct if r not in far]
    off = topo.engines(c, T.cores[far[0]])
    on = [e for e in topo.engines(c, via[0][0]) if e not in off]
    n, m = len(off) // len(far), len(on) // len(via)
    plan = {r: off[i * n:(i + 1) * n] for i, r in enumerate(far)}
    xplan = dict(plan)
    for r in near:
        plan[r] = on[:m]
        xplan[r] = on[0:1]
    (a, b), (d, e) = via[0][1], via[1][1]
    xplan.update({a: on[1:2], b: on[2:4], d: on[4:6], e: on[6:8]})
    return plan, [on[i * m:(i + 1) * m] for i in range(len(via))], xplan


def helper_engines(T, topo, h, rs):
    es = topo.engines(h, T.cores[rs[0]])
    n = len(es) // len(rs)
    return [es[i * n:(i + 1) * n] for i in range(len(rs))]


def dst(topo, d, s):
    rid, pid = topo.addr(d, s)
    return DstId(rid=rid, pnc=pid)


def helper_program(g, core, T, topo, rank, rs, n_in, n_x):
    es = helper_engines(T, topo, core, rs)
    here = slice(rank * 64, rank * 64 + 64)
    for src, to, arr, h, n in (([T.xh[0], T.xh[1]], T.xl[rank], T.sem.arr0, T.sem.h0, n_x),
                               ([T.ha[:, 0:64], T.ha[:, 64:128]], T.la[:, here], T.sem.arr1, T.sem.h1, n_in),
                               ([T.hz[:, 0:64], T.hz[:, 64:128]], T.lz[:, here], T.sem.arr2, T.sem.h2, n_in)):
        g.wait_ge(h, n)
        g.remote_dma_fused([RemoteDMATransfer(dst_ids=[dst(topo, T.cores[r], core)], dma_engine_mask=bits(es[i]), remote_sem=arr,
                                              src=src[i], dst=to) for i, r in enumerate(rs)], local_sem=T.sem.sent)
    g.wait_ge(T.sem.sent, 3 * sum(len(e) for e in es))


def build(g, core, T, topo, rank):
    ops = []
    state = {}
    rts = routes(T, topo)
    direct, via = rts[rank]
    plan, hplan, xplan = engine_plan(T, topo, rank, direct, via)
    n_arr = n_arx = 0
    for s in range(N):
        if s == rank:
            continue
        ds, vs = rts[s]
        if rank in ds:
            p = engine_plan(T, topo, s, ds, vs)
            n_arr += len(p[0][rank])
            n_arx += len(p[2][rank])
        else:
            h, rs = [e for e in vs if rank in e[1]][0]
            n_arr += len(helper_engines(T, topo, h, rs)[rs.index(rank)])
            n_arx += len(helper_engines(T, topo, h, rs)[rs.index(rank)])
    pb = [T["pb%d" % b] for b in range(8)]

    def op(eng, cost, rd, wr, fn, bank=None, done=None, lag=0.0):
        me = len(ops)
        rd, wr = rd.split(), wr.split()
        deps = set()
        for k in rd + wr:
            st = state.setdefault(k, [None, []])
            if st[0] is not None:
                deps.add(st[0])
        for k in wr:
            deps.update(state[k][1])
        for k in rd:
            state[k][1].append(me)
        for k in wr:
            state[k] = [me, []]
        deps.discard(me)
        ops.append({"eng": eng, "cost": cost, "deps": deps, "fn": fn, "bank": bank, "done": done, "lag": lag, "wr": (wr + ["-"])[0]})

    def vc(n, f=1.0):
        return 50.0 + max(64.0, n * f)

    def ts(out, in0, s1, s2, o0, o1, n, rd, wr, bank=None, f=1.0):
        if o1 is None:
            op("v", vc(n, f), rd, wr, lambda: g.vector.tensor_scalar(out, in0, s1, None, o0), bank)
        else:
            op("v", vc(n, f), rd, wr, lambda: g.vector.tensor_scalar(out, in0, s1, s2, o0, o1), bank)

    def tt(out, a, b, o, n, rd, wr, bank=None):
        op("v", vc(n, 2.0 if bank is None else 1.0), rd, wr, lambda: g.vector.tensor_tensor(out, a, b, o), bank)

    def cp(out, a, n, rd, wr, bank=None, f=1.0):
        op("v", vc(n, f), rd, wr, lambda: g.vector.tensor_copy(out, a), bank)

    def ms(out, c, n, wr):
        op("v", vc(n), "", wr, lambda: g.vector.memset(out, c))

    def scan(out, d0, d1, init, o0, o1, n, rd, wr, bank=None, f=1.0):
        op("v", vc(n, f), rd, wr, lambda: g.vector.tensor_tensor_scan(out, d0, d1, init, o0, o1), bank)

    def act(out, a, func, n, rd, wr, bank=None, f=1.0, bias=0.0, scale=1.0, extra=0.0):
        op("a", 65.0 + extra + max(64.0, n * f), rd, wr, lambda: g.scalar.activation(out, a, func, bias=bias, scale=scale), bank)

    def iota(out, pat, n, rd, wr, real=True):
        if real:
            op("g", 130.0 + 2 * n, rd, wr, lambda: g.iota(out, pat, 0, 0, allow_small_or_imprecise_dtypes=True))
        else:
            op("g", 130.0 + 2 * n, rd, wr, lambda: g.iota(out, pat, 0, 0))

    def asel(out, a, pat, o, fill, base, cm, n, rd, wr):
        op("g", 170.0 + 2 * n, rd, wr, lambda: g.affine_select(out, a, pat, o, fill, base, cm))

    def mm(items, rd, wr, bank):
        def fn():
            for o, l, r, s, e, n in items:
                last = g.tensor.matmul(o, l, r, s, e)
            return last
        op("p", 60.0 + 0.5 * sum(max(64, i[5]) for i in items), rd, wr, fn, bank)

    def group(out, terms, n):
        return [(out, l, r, i == 0, i == len(terms) - 1, n) for i, (l, r) in enumerate(terms)]

    def keys(name, n):
        return " ".join("%s%d" % (name, i) for i in range(n)) + " "

    def blocks(t, w, n):
        return [t[:, w * i:w * i + w] for i in range(n)]

    GA, SC = 1.56, 3.8
    ADD, SUB, MUL, MAX, MIN, EQ = ALU.add, ALU.subtract, ALU.mult, ALU.max, ALU.min, ALU.is_equal
    here = slice(rank * 64, rank * 64 + 64)
    op("s", 60.0, "", "sin", lambda: g.sync.dma_start(T.sin[:], T.stars[:]).then_inc(T.sem.lds, 16), done=("lds", 16), lag=2200.0)
    op("a", 60.0, "", "xs", lambda: g.scalar.dma_start(T.xs[:], T.x[:]).then_inc(T.sem.ldx, 16), done=("ldx", 16), lag=2000.0)
    ms(T.ones[:], 1.0, 64, "ones")
    I = T.ii[:, 0:128]
    asel(I, T.ones[:], [[-1, 128]], EQ, 0.0, 0, 1, 128, "ones", "ii")
    op("g", 170.0, "", "pi", lambda: g.iota(T.pi[:], [[1, 16]], 0, 1))
    iota(T.mlo[:], [[0, 9], [1, 16]], 144, "", "mlo")
    iota(T.mhi[:], [[1, 8], [0, 16]], 128, "", "mhi")
    iota(T.mf[:], [[1, 144]], 144, "", "mf")

    def send_x():
        g.remote_dma_fused([RemoteDMATransfer(dst_ids=[dst(topo, h, core)], dma_engine_mask=bits(xplan[r]), remote_sem=T.sem.h0,
                                              src=T.xs[r], dst=T.xh[i]) for h, rs in via for i, r in enumerate(rs)]
                           + [RemoteDMATransfer(dst_ids=[dst(topo, T.cores[r], core)], dma_engine_mask=bits(xplan[r]), remote_sem=T.sem.arr0,
                                                src=T.xs[r], dst=T.xl[rank]) for r in direct], local_sem=T.sem.sent)
    op("g", 1000.0, "xs ii pi mlo mhi mf", "sent0", send_x, done=())
    op(None, 6000.0, "sent0", "xl", None, done=("arr0", n_arx))
    ts(T.s16[:], T.sin[:], -SH, None, ADD, None, 512, "sin", "s16")
    mm([(pb[0][:, j::4], T.s16[:, 128 * j:128 * j + 128], I, True, True, 128) for j in range(4)], "s16 ii", "b0", 0)
    cp(T.pa[:], pb[0][:], 512, "b0", "pa", 0)

    def send(src, land, to, hsem, arr):
        def fn():
            g.remote_dma_fused([RemoteDMATransfer(dst_ids=[dst(topo, h, core)], dma_engine_mask=bits(hplan[i]), remote_sem=hsem,
                                                  src=src[:, rs[0] * 64:(rs[0] + 2) * 64], dst=land[:])
                                for i, (h, rs) in enumerate(via)], local_sem=T.sem.sent)
            g.remote_dma_fused([RemoteDMATransfer(dst_ids=[dst(topo, T.cores[r], core)], dma_engine_mask=bits(plan[r]), remote_sem=arr,
                                                  src=src[:, r * 64:(r + 1) * 64], dst=to[:, here])
                                for r in direct], local_sem=T.sem.sent)
        return fn
    n_sent = 2 * (sum(len(e) for e in hplan) + sum(len(plan[r]) for r in direct)) + sum(len(e) for e in xplan.values())
    op("g", 1000.0, "pa sent0", "sent1", send(T.pa, T.ha, T.la, T.sem.h1, T.sem.arr1), done=())
    cp(T.la[:, here], T.pa[:, here], 64, "pa", "laown", f=0.5)
    op(None, 5000.0, "sent1", "la", None, done=("arr1", n_arr))
    P, PHI, CORB, CORS, NCEN, DV, A48, N48, WQ, WDC, W0, FB0, DV0 = blocks(T.pc, 1, 13)
    PLO, ORD1 = T.plc[:, 0:1], T.plc[:, 11:12]
    cp(P, T.pi[:, 0:1], 1, "pi", "P")
    ts(T.pj[:], T.pi[:], 15, None, ALU.bitwise_and, None, 16, "pi", "pj")
    cp(T.plc[:], T.pj[:], 16, "pj", "plc")
    ts(PHI, P, PLO, 0.0625, SUB, MUL, 1, "P plc", "PHI")
    ts(T.jj[:], T.mhi[:], PHI, None, EQ, None, 128, "mhi PHI", "jj")
    ts(T.km[:], T.mlo[:, 0:128], PLO, None, EQ, None, 128, "mlo plc", "km")
    ts(T.gmask[:], T.mf[:, 0:8], PHI, None, EQ, None, 8, "mf PHI", "gmask")
    ts(T.kmask[:], T.mf[:, 0:16], PLO, None, EQ, None, 16, "mf plc", "kmask")
    cp(T.gsel[:], T.gmask[:], 8, "gmask", "gsel")
    REP, SEL, PM, CK = blocks(T.rep, 128, 8), blocks(T.sel, 128, 16), blocks(T.pm, 128, 4), blocks(T.ck, 128, 3)
    LTS, LIS = blocks(T.lt, 128, 2), blocks(T.li, 128, 2)
    for r in range(8):
        act(REP[r], T.km[:], ACT.Copy, 128, "km gmask", "rep%d" % r, scale=T.gmask[:, r:r + 1])
    for k in range(16):
        ts(SEL[k], T.jj[:], T.kmask[:, k:k + 1], None, MUL, None, 128, "jj kmask", "sel%d" % k, f=0.5)
    act(T.ii[:, 128:256], I, ACT.Copy, 128, "ii", "ii2")
    for name, src, c in (("ineg", "ii", -1.0), ("ibig", "ii", 4096.0), ("j9", "jj", 9.0), ("jbig", "jj", 4096.0), ("jnbig", "jj", -4096.0)):
        act(T[name][:], T[src][:, 0:128], ACT.Copy, 128, src, name, scale=c)
    for col, name, src, sn, a, b in ((CORS, "CORS", PLO, "plc", -BIG, 15 * BIG - 9.0), (CORB, "CORB", PLO, "plc", -BIG, 15 * BIG - 30 * SH),
                                     (NCEN, "NCEN", PLO, "plc", -512.0, -255.5 - 30 * SH), (A48, "A48", PHI, "PHI", 48.0, 0.0),
                                     (N48, "N48", PHI, "PHI", -48.0, 0.0), (WDC, "WDC", PHI, "PHI", 16.0, 15.0),
                                     (W0, "W0", PHI, "PHI", 512.0, -SH)):
        ts(col, src, a, b, MUL, ADD, 1, sn, name)
    ts(FB0, PHI, 560.0, PLO, MUL, ADD, 1, "PHI plc", "FB0")
    ts(T.pk[:, 0:1], PHI, PLO, 8.0, SUB, ADD, 1, "PHI plc", "pk0")
    ts(T.pk[:, 1:2], T.pk[:, 0:1], 7, None, ALU.bitwise_and, None, 1, "pk0", "pk1")
    cp(DV0, T.pk[:, 1:2], 1, "pk1", "DV0")
    ts(WQ, PLO, 8.0, 8.0, EQ, MUL, 1, "plc", "WQ")
    ts(DV, DV0, WQ, None, MAX, None, 1, "DV0 WQ", "DV")
    act(T.dm[:], T.jj[:], ACT.Copy, 128, "jj DV", "dm", scale=DV)
    ts(T.wd[:], T.mf[:], WDC, None, EQ, None, 144, "mf WDC", "wd")
    act(T.wd2[:], T.wd[:], ACT.Copy, 144, "wd", "wd2", scale=2.0)
    for h in range(2):
        act(T.rd[:, 128 * h:128 * h + 128], T.km[:], ACT.Identity, 128, "km", "rd%d" % h, scale=HUGE + BIG, bias=-BIG)
    act(T.fb[:], T.mf[:, 0:32], ACT.Identity, 32, "mf FB0", "fb", scale=16.0, bias=FB0)
    ts(T.tmpb[:], T.mlo[:, 0:128], 8.0, -1.0, ALU.is_ge, MUL, 128, "mlo", "tmpb")
    tt(T.jhi[:], T.tmpb[:], T.jj[:], MUL, 128, "tmpb jj", "jhi")
    for i in range(4):
        asel(PM[i], T.ones[:], [[-16, 8], [-256, 2], [-1, 8]], EQ, 0.0, 256 * (i % 2) - 8 * (i // 2), 1, 128, "ones sent1", "pm%d" % i)
    iota(T.tf[:], [[2, 256]], 256, "sent1", "tf")
    asel(LTS[0], T.jbig[:], [[1, 128]], ALU.is_gt, 0.0, 0, -1, 128, "jbig sent1", "lt0")
    ts(T.tmpb[:], T.mlo[:, 11:139], ORD1, None, ALU.is_gt, None, 128, "mlo plc", "tmpb")
    tt(LTS[1], T.tmpb[:], T.jbig[:], MUL, 128, "tmpb jbig", "lt1")
    for t in range(RO):
        asel(LIS[t], LTS[t], [[1, 128]], ALU.not_equal, -4096.0, 0, -1, 128, "lt%d sent1" % t, "li%d" % t)
        ts(T.wn[:, 256 * t:256 * t + 256], T.tf[:], W0, float(t), ADD, ADD, 256, "tf W0", "wn%d" % t)
    asel(T.shm[:], T.jj[:], [[-1, 128]], EQ, 0.0, -1, 1, 128, "jj sent1", "shm")
    asel(T.shm[:, 15::16], T.jj[:, 15::16], [[-16, 8]], EQ, 0.0, 0, 1, 8, "jj", "shm")
    asel(T.ish[:], T.shm[:], [[-1, 128]], ALU.not_equal, 1.0, 0, 1, 128, "shm", "ish")
    iota(T.ti[:, 0:128], [[512, 8], [1, 16]], 128, "sent1", "ti0", False)
    iota(T.ti[:, 128:160], [[16, 32]], 32, "sent1", "ti1", False)
    cp(T.chi[:], T.ti[:, 0:128], 128, "ti0", "chi")
    cp(T.clo[:], T.ti[:, 128:160], 32, "ti1", "clo")
    for i, c in enumerate((-16.0, -464.0, 256.0)):
        ms(CK[i], c, 64, "ck%d" % i)
    ms(T.zero[:], 0.0, 128, "zero")
    ms(T.sw[:, 4480:4488], SH, 8, "sw8")
    ms(T.xw[:, 4096:4112], FAR, 16, "xw8")
    ms(T.ns[:, 0:432], 0.0, 432, "ns")
    ONE = T.ones[:, 0:64]
    R = [T.wd[:, 15 - k:143 - k] for k in range(16)]
    R2 = R[0:8] + [T.wd2[:, 15 - k:143 - k] for k in range(8, 16)]
    SW, XW = keys("sw", 9), "xw xw8 "
    swin, xwin = T.sw[:, 384:4488], T.xw[:, 0:4112]
    nat = [T.nat0, T.nat1, T.nat2]
    mm([(pb[0][:, 128 * j:128 * j + 128], T.la[:, j::4], I, True, True, 128) for j in range(4)], "la laown ii", "b0", 0)
    cp(T.nat0[:], pb[0][:], 512, "b0", "nat0", 0)

    def x_out():
        for r in range(8):
            g.sync.dma_start(T.dx[:, 512 * r:512 * r + 512], T.xs[r] if r == rank else T.xl[r]).then_inc(T.sem.dx1, 16)

    def x_in():
        for r in range(8):
            g.sync.dma_start(T.xw[16 * r:16 * r + 16, 0:4096], T.dx[:]).then_inc(T.sem.dx2, 16)
    op("s", 800.0, "xs xl", "dx", x_out, done=("dx1", 128), lag=2500.0)
    op("s", 800.0, "dx", "xw", x_in, done=("dx2", 128), lag=7000.0)

    def halves(j):
        return ([slice(1024 * j + 512 * h, 1024 * j + 512 * h + 512) for h in range(2)],
                [slice(1024 * j + 512 * (k // 8) + k % 8, 1024 * j + 512 * (k // 8) + 512, 8) for k in range(16)])

    for t in range(RO):
        nk = "nat%d " % t
        wk = "wn%d " % t
        LT, LI = LTS[t], LIS[t]
        for r in range(8):
            b = (r + 1) % 4
            o = T.sw[:, 384 + 512 * r:896 + 512 * r]
            mm([(pb[b][:], REP[r], nat[t][:], True, True, 512)], nk + "rep%d" % r, "b%d" % b, b)
            if r % 2 == 0:
                act(o, pb[b][:], ACT.Copy, 512, "b%d" % b, "sw%d" % r, b)
            else:
                cp(o, pb[b][:], 512, "b%d" % b, "sw%d" % r, b)
        mm(sum([group(pb[7][:, 128 * h:128 * h + 128], [(PM[2 * h + e], nat[t][:, t + 2 * e::4]) for e in range(2)], 128) for h in range(2)], []),
           keys("pm", 4) + nk, "b7", 7)
        ts(T.off[:], pb[7][:, 0:256], SH, None, ADD, None, 256, "b7", "off", 7)
        ts(T.ni[:], nat[t][:, t::2], SH, None, EQ, None, 256, nk, "ni", f=0.5)
        fill = [0]
        for j in range(NCH):
            u = slice(U * j, U * j + U)
            c = "%d " % j
            hs, ks = halves(j)
            sa = nat[t][:, t + 2 * U * j:2 * U * (j + 1):2]
            wn = T.wn[:, 256 * t + U * j:256 * t + U * j + U]
            za, zb = T.za[:, u], T.zb[:, u]
            for h in range(2):
                act(T.gs[:, hs[h]], swin.indirect(T.off[:, 128 * h + 32 * j:128 * h + 32 * j + 32]), ACT.Copy, 512, SW + "off", "gs%d%d" % (j, h), f=GA)
            b = fill[0] % 2
            fill[0] += 1
            mm([(pb[b][:, k::8], I, wn, True, True, U) for k in range(8)], "ii " + wk, "b%d" % b, b)
            for h in range(2):
                tt(T.eqw[:, hs[h]], T.gs[:, hs[h]], pb[b][:], EQ, 512, "gs%d%d b%d" % (j, h, b), "eqw%d%d" % (j, h), b)
            mm(group(pb[4][:, 0:64], [(I, T.ni[:, u])] + [(R[k], T.eqw[:, ks[k]]) for k in range(16)], U),
               "eqw%d0 eqw%d1 wd ni" % (j, j), "h", 4)
            ts(za, pb[4][:, 0:64], 0.0, None, EQ, None, U, "h", "za" + c, 4)
            for h in range(2):
                b = fill[0] % 2
                fill[0] += 1
                mm([(pb[b][:, k::8], SEL[(8 * h + k + 1) % 16], sa, True, True, U) for k in range(8)], keys("sel", 16) + nk, "b%d" % b, b)
                tt(T.eqc[:, hs[h]], T.gs[:, hs[h]], pb[b][:], EQ, 512, "gs%d%d b%d" % (j, h, b), "eqc%d%d" % (j, h), b)
            mm(group(pb[4][:, 64:128], [(T.ish[:], T.ni[:, u]), (I, za)] + [(R[k], T.eqc[:, ks[k]]) for k in range(16)], U),
               "eqc%d0 eqc%d1 wd ni ish za%d" % (j, j, j), "h2", 4)
            ts(zb, pb[4][:, 64:128], 0.0, None, EQ, None, U, "h2", "zb" + c, 4)
            mm(group(pb[4][:, 128:192], [(I, sa), (LI, za), (LI, zb)], U) + group(pb[4][:, 192:256], [(I, wn), (LI, za), (LT, zb)], U)
               + group(pb[4][:, 256:320], [(T.shm[:], sa), (LT, za), (LI, zb)], U),
               nk + wk + "za%d zb%d lt%d li%d shm" % (j, j, t, t), "p", 4)
            ts(T.val[:, :, u], pb[4][:, 128:320], 4096.0, SH, ADD, MIN, 192, "p", "val" + c, 4)
            mm(group(pb[5][:, 128 * j:128 * j + 64], [(CK[2], ONE), (T.jj[:], T.val[:, 0, u])], U)
               + group(pb[5][:, 128 * j + 64:128 * j + 128], [(T.jj[:], T.val[:, 1, u]), (T.jj[:], T.val[:, 2, u])], U),
               "jj ck2 ones val" + c, "bz" + c, 5)
            scan(T.dsc[:, 128 * j:128 * j + 128], T.rd[:, 0:128], pb[5][:, 128 * j:128 * j + 128], 0.0, ADD, MIN, 128, "rd0 bz" + c, "dsc" + c, 5)
            ts(T.obz[:, 8 * j:8 * j + 8], T.dsc[:, 128 * j + 15:128 * j + 128:16], CORB, None, ADD, None, 8, "CORB dsc" + c, "obz" + c)
            act(T.dab[:, u], pb[5][:, 128 * j:128 * j + 64], ACT.Abs, U, "NCEN bz" + c, "dab" + c, 5, bias=NCEN)
        DAB, VAL, BZ = keys("dab", NCH), keys("val", NCH), keys("bz", NCH)
        act(T.sg[:], T.dab[:], ACT.Sign, 256, DAB, "sg", bias=256.0, scale=-1.0)
        act(T.ind[:], T.sg[:], ACT.Relu, 256, "sg", "ind")
        act(T.fac[:], T.sg[:], ACT.Identity, 256, "sg", "fac", bias=(1 + INVB) / 2, scale=-(1 - INVB) / 2)
        scan(pb[5][:, 0:256], T.fac[:], T.zero[:], 1.0, MUL, ADD, 256, "fac zero", "bz0 bz1", 5)
        scan(pb[5][:, 256:512], T.ind[:], T.zero[:], 0.0, ADD, ADD, 256, "ind zero", "bz2 bz3", 5)
        tt(T.wsel[:], T.ind[:], pb[5][:, 0:256], MUL, 256, "ind bz0 bz1", "wsel", 5)
        tt(T.csel[:], T.ind[:], pb[5][:, 256:512], MUL, 256, "ind bz2 bz3", "csel", 5)
        mm(group(pb[7][:, 0:256], [(T.dm[:], T.ind[:]), (T.j9[:], T.csel[:])], 256), "dm j9 ind csel", "b7", 7)
        scan(T.ssc[:], T.rd[:], pb[7][:, 0:256], 0.0, ADD, MIN, 256, "b7 rd0 rd1", "ssc", 7)
        ts(T.slot[:], T.ssc[:, 15::16], CORS, None, ADD, None, 16, "ssc CORS", "slot")
        mm([(pb[7][:, 256 + 8 * h:264 + 8 * h], T.val[:, 0, 128 * h:128 * h + 128], T.gsel[:], True, True, 8) for h in range(2)],
           VAL + "gsel", "bt", 7)
        ts(T.bti[:], pb[7][:, 256:272], -14 * SH, None, ADD, None, 16, "bt", "bti", 7)
        ts(T.btm[:, 0:16], T.bti[:], 0x1E0F, None, ALU.bitwise_and, None, 16, "bti", "btm0")
        ts(T.btm[:, 16:32], T.bti[:], 0x1F0, None, ALU.bitwise_and, None, 16, "bti", "btm1")
        cp(T.btf[:], T.btm[:], 32, "btm0 btm1", "btf")
        mm([(pb[7][:, 272 + 8 * h:280 + 8 * h], T.wsel[:, 128 * h:128 * h + 128], T.gsel[:], True, True, 8) for h in range(2)],
           "wsel gsel", "wtp", 7)
        act(T.wtt[:], pb[7][:, 272:288], ACT.Copy, 16, "wtp", "wtt", 7)
        OH, OL = blocks(T.ohh, 128, 16), blocks(T.ohl, 32, 16)
        for i in range(16):
            ts(OH[i], T.chi[:], T.btf[:, i:i + 1], None, EQ, None, 128, "chi btf", "ohh%d" % i, f=0.5)
            ts(OL[i], T.clo[:], T.btf[:, 16 + i:17 + i], T.wtt[:, i:i + 1], EQ, MUL, 32, "clo btf wtt", "ohl%d" % i, f=0.5)
        tab = [(pb[5][:, 0:288:9], OH[0], OL[0], True, True, 32)]
        for q in range(8):
            tab += group(pb[5][:, 8 - q:288:9], [(OH[i], OL[i]) for i in (q, 8 + q)], 32)
        mm(tab, keys("ohh", 16) + keys("ohl", 16), BZ, 5)
        act(T.lg[:], pb[5][:, 0:288], ACT.Ln, 288, BZ, "lg", 5, bias=2.0 ** -63, scale=math.exp(0.69 * LNB), extra=1300.0 * (t == 0))
        act(T.rr[:], T.lg[:], ACT.Identity, 288, "lg", "rr", bias=MAGIC, scale=-1.0 / LNB)
        ts(T.kp[:], T.rr[:], -MAGIC, 48.0, ADD, MIN, 288, "rr", "kp")
        act(T.ke[:], T.kp[:], ACT.Relu, 288, "kp", "ke", bias=-47.0)
        act(T.kp[:, 0::9], T.fb[:], ACT.Copy, 32, "fb", "kp")
        act(T.ke[:, 0::9], T.zero[:, 0:32], ACT.Copy, 32, "zero", "ke")
        scan(T.ks[:], T.ke[:], T.kp[:], 0.0, MUL, ADD, 288, "ke kp", "ks")
        ts(T.t2[:], T.ks[:, 8::9], A48, 384.0, ALU.is_lt, MUL, 32, "ks A48", "t2")
        tt(T.t3[:], T.ks[:, 8::9], T.t2[:], ADD, 32, "ks t2", "t3")
        ts(T.key[:], T.t3[:], N48, None, ADD, None, 32, "t3 N48", "key")
        for j in range(NCH):
            u = slice(U * j, U * j + U)
            c = "%d " % j
            hs, ks = halves(j)
            ob, obz = T.obz[:, 8 * j:8 * j + 4], T.obz[:, 8 * j:8 * j + 8]
            xb, xz = T.xbz[:, 128 * j:128 * j + 64], T.xbz[:, 128 * j + 64:128 * j + 128]
            blk, fr = T.blk[:, u], T.fr[:, u]
            cp(T.e16[:, u], swin.indirect(ob), U, SW + "obz" + c, "e16" + c, f=GA)
            mm(sum([group(pb[4][:, 320 + 32 * h:352 + 32 * h], [(PM[2 * h + e], T.e16[:, U * j + e:U * j + U:2]) for e in range(2)], 32)
                    for h in range(2)], []), keys("pm", 4) + "e16" + c, "eop", 4)
            ts(T.eo[:, u], pb[4][:, 320:384], SH, None, ADD, None, U, "eop", "eo" + c, 4)
            act(T.xbz[:, 128 * j:128 * j + 128], xwin.indirect(obz), ACT.Copy, 128, XW + "obz" + c, "xbz" + c, f=GA)
            for h in (1, 0):
                act(T.gx[:, hs[h]], xwin.indirect(T.eo[:, U * j + 32 * h:U * j + 32 * h + 32]), ACT.Copy, 512, XW + "eo" + c, "gx%d%d" % (j, h), f=GA)
            ts(T.dead[:, u], T.e16[:, u], SH, 2.0, EQ, MUL, U, "e16" + c, "dead" + c, f=0.5)
            mm(group(pb[4][:, 384:448], [(I, xb), (T.ineg[:], xz)], U), "ii ineg xbz" + c, "zbp", 4)
            act(T.mzb[:, u], pb[4][:, 384:448], ACT.Abs, U, "zbp", "mzb" + c, 4)
            for i, (xx, out, name) in enumerate(((xz, T.az, "az"), (xb, T.ab, "ab"))):
                b, d = (3, 2) if j < 2 or i == 0 else (1, 0)
                mm([(pb[b][:, k::8], I, xx, True, True, U) for k in range(8)], "ii xbz" + c, "b%d" % b, b)
                tt(out[:, hs[1]], T.gx[:, hs[1]], pb[b][:], MAX, 512, "gx%d1 b%d" % (j, b), "%s%d1" % (name, j), b)
                mm([(pb[d][:], T.ineg[:], T.gx[:, hs[0]], True, False, 512)] + [(pb[d][:, k::8], I, xx, False, k == 7, U) for k in range(8)],
                   "ii ineg gx%d0 xbz%d" % (j, j), "b%d" % d, d)
                act(out[:, hs[0]], pb[d][:], ACT.Abs, 512, "b%d" % d, "%s%d0" % (name, j), d)
            mm(group(pb[6][:, 128:192], [(T.jj[:], T.mzb[:, u])] + [(R[k], T.gx[:, ks[k]]) for k in range(8, 16)], U),
               "wd jj gx%d1 mzb%d" % (j, j), "accs", 6)
            mm(group(pb[6][:, 0:64], [(T.jhi[:], xz)] + [(R2[k], T.az[:, ks[k]]) for k in range(16)], U),
               "wd wd2 jhi az%d0 az%d1 xbz%d" % (j, j, j), "acce", 6)
            act(T.ae[:, u], pb[6][:, 0:64], ACT.Copy, U, "acce", "ae" + c, 6)
            tt(blk, T.ae[:, u], pb[6][:, 128:192], ALU.is_lt, U, "accs ae" + c, "blk" + c, 6)
            mm(group(pb[6][:, 64:128], [(T.jhi[:], xb), (T.ibig[:], T.dead[:, u])] + [(R2[k], T.ab[:, ks[k]]) for k in range(16)], U),
               "wd wd2 jhi ibig ab%d0 ab%d1 xbz%d dead%d" % (j, j, j, j), "accb", 6)
            tt(fr, T.ae[:, u], pb[6][:, 64:128], ALU.is_lt, U, "accb ae" + c, "fr" + c, 6)
            mm(group(pb[6][:, 192:256], [(CK[0], ONE), (T.jnbig[:], blk), (T.ibig[:], fr)], U)
               + group(pb[6][:, 256:320], [(CK[1], ONE), (T.jj[:], T.val[:, 1, u]), (T.jj[:], T.val[:, 2, u]), (T.jbig[:], blk), (LIS[0], fr)], U),
               "ck0 ck1 ones jnbig jbig ibig li0 jj val%d blk%d fr%d" % (j, j, j), "p12", 6)
            tt(T.keep[:, u], T.e16[:, u], pb[6][:, 192:256], MAX, U, "p12 e16" + c, "keep" + c, 6)
            tt(T.nn[:, u], T.keep[:, u], pb[6][:, 256:320], MIN, U, "p12 keep" + c, "nn" + c, 6)
            cp(T.ns[:, 0:2320].indirect(T.slot[:, 4 * j:4 * j + 4]), T.nn[:, u], U, "slot nn" + c, "ns", f=SC)
        cp(T.cv[:], T.ns[:, 0:432], 432, "ns", "cv")
        mm([(pb[7][:, 48 * d:48 * d + 48], T.ii[:, 16 * d:16 * d + 128], T.cv[:, d::9], True, True, 48) for d in range(8)],
           "cv ii ii2", "b7 bt wtp", 7)
        act(T.sw[:, 0:384], pb[7][:, 0:384], ACT.Copy, 384, "b7 bt wtp", "nwn", 7)
        cp(nat[t + 1][:], T.sw[:, 0:4488].indirect(T.key[:]), 512, SW + "nwn key", "nat%d" % (t + 1), f=GA)
    mm([(pb[0][:, j::4], T.nat2[:, 128 * j:128 * j + 128], I, True, True, 128) for j in range(4)], "nat2 ii", "b0", 0)
    cp(T.pz[:], pb[0][:], 512, "b0", "pz", 0)
    op("g", 1000.0, "pz", "sent2", send(T.pz, T.hz, T.lz, T.sem.h2, T.sem.arr2), done=())
    cp(T.lz[:, here], T.pz[:, here], 64, "pz", "lzown", f=0.5)
    op(None, 5000.0, "sent2", "lz", None, done=("arr2", n_arr))
    for h in range(2):
        mm([(pb[1 + h][:, 128 * j:128 * j + 128], T.lz[:, 2 * h + j::4], I, True, True, 128) for j in range(2)], "lz lzown ii", "b%d" % (1 + h), 1 + h)
    ts(T.yo[:, 0:256], pb[1][:, 0:256], SH, None, ADD, None, 256, "b1", "yo0", 1)
    op("s", 60.0, "yo0", "", lambda: g.sync.dma_start(T.y[:, 0:256], T.yo[:, 0:256]).then_inc(T.sem.st0, 16), done=("st0", 16), lag=2000.0)
    act(T.yo[:, 256:512], pb[2][:, 0:256], ACT.Identity, 256, "b2", "yo1", 2, bias=SH)
    op("a", 60.0, "yo1", "", lambda: g.scalar.dma_start(T.y[:, 256:512], T.yo[:, 256:512]).then_inc(T.sem.st1, 16), done=("st1", 16), lag=2000.0)
    return ops, n_sent


def schedule(ops, bump, slack=60.0):
    n = len(ops)
    succ = [[] for _ in range(n)]
    for i, o in enumerate(ops):
        for d in o["deps"]:
            succ[d].append(i)
    prio = [0.0] * n
    for i in range(n - 1, -1, -1):
        prio[i] = ops[i]["cost"] + ops[i]["lag"] + max([prio[s] + LAT for s in succ[i]] + [0.0])
    prio = [a + b for a, b in zip(prio, bump)]
    left = [len(o["deps"]) for o in ops]
    ready = [i for i in range(n) if left[i] == 0]
    end, start, dep_t = [0.0] * n, [0.0] * n, [0.0] * n
    free, users, order = {}, {}, []
    extra = [set() for _ in range(n)]

    def est(i):
        o = ops[i]
        t = max(dep_t[i], free.get(o["eng"], 0.0))
        for e, k in users.get(o["bank"], {}).items():
            if e != o["eng"]:
                t = max(t, end[k] + LAT)
        return t
    while ready:
        es = {i: est(i) for i in ready}
        first = min(ready, key=lambda i: (es[i], -prio[i]))
        eng = ops[first]["eng"]
        i = max([k for k in ready if ops[k]["eng"] == eng and es[k] <= es[first] + slack], key=lambda k: prio[k])
        o = ops[i]
        start[i] = es[i]
        end[i] = es[i] + o["cost"] + o["lag"]
        if eng:
            free[eng] = es[i] + o["cost"]
        if o["bank"] is not None:
            us = users.setdefault(o["bank"], {})
            extra[i].update(k for e, k in us.items() if e != eng)
            us[eng] = i
        ready.remove(i)
        order.append(i)
        for s in succ[i]:
            left[s] -= 1
            dep_t[s] = max(dep_t[s], end[i] + LAT)
            if left[s] == 0:
                ready.append(s)
    return order, extra, start, end


def best_schedule(ops, tries=5000):
    n = len(ops)
    seed = [7]

    def rnd(m):
        seed[0] = (seed[0] * 1103515245 + 12345) % 2147483648
        return (seed[0] >> 8) % m
    bump = [3000.0 if o["cost"] < 420 else 0.0 for o in ops]
    best = schedule(ops, bump)
    keep = best
    for _ in range(tries):
        b = list(bump)
        for _k in range((1, 2, 4)[rnd(3)]):
            i, w, d = rnd(n), (1, 1, 3, 8, 20)[rnd(5)], (rnd(2001) - 1000) * (1.0, 3.0, 8.0)[rnd(3)]
            for x in range(i, min(n, i + w)):
                b[x] += d
        r = schedule(ops, b)
        if max(r[3]) <= max(best[3]) + 30.0:
            best, bump = r, b
            if max(r[3]) < max(keep[3]):
                keep = r
    return keep


CACHE = {}


def rank_program(g, core, T, topo):
    rank = T.rank_of(core)
    if rank is None:
        for r, (direct, via) in enumerate(routes(T, topo)):
            for i, (h, rs) in enumerate(via):
                if h == core:
                    p = engine_plan(T, topo, r, direct, via)
                    helper_program(g, core, T, topo, r, rs, len(p[1][i]), sum(len(p[2][k]) for k in rs))
        return
    ops, n_sent = build(g, core, T, topo, rank)
    if "s" not in CACHE:
        CACHE["s"] = best_schedule(ops)
    order, extra = CACHE["s"][0:2]
    queue = {"v": g.vector, "a": g.scalar, "p": g.tensor, "g": g, "s": g.sync}
    count = {k: 0 for k in QSEM}
    waited = {k: {} for k in queue}
    done = {}
    for i in order:
        o = ops[i]
        eng = o["eng"]
        if eng is None:
            done[i] = o["done"]
            continue
        need = {}
        for d in set(o["deps"]) | extra[i]:
            if not done[d] or (eng == "p" and ops[d]["eng"] == "p"):
                continue
            s, v = done[d]
            need[s] = max(need.get(s, 0), v)
        for s, v in sorted(need.items()):
            if waited[eng].get(s, 0) < v:
                queue[eng].wait_ge(T.sem[s], v)
                waited[eng][s] = v
        ins = o["fn"]()
        if o["done"] is None:
            count[eng] += 1
            ins.then_inc(T.sem[QSEM[eng]], 1)
            done[i] = (QSEM[eng], count[eng])
        else:
            done[i] = o["done"]
    for k, s in QSEM.items():
        g.wait_ge(T.sem[s], count[k])
    g.wait_ge(T.sem.sent, n_sent)
    g.wait_ge(T.sem.st0, 16)
    g.wait_ge(T.sem.st1, 16)
